import numpy as np
import ml_dtypes


def mxq(x, axis, fmt="e4m3"):
    dtype, down = {"e4m3": (ml_dtypes.float8_e4m3fn, 7), "e5m2": (ml_dtypes.float8_e5m2, 14)}[fmt]
    v = np.moveaxis(np.asarray(x, np.float32).astype(ml_dtypes.bfloat16).astype(np.float64), axis, -1)
    blocks = v.reshape(v.shape[:-1] + (-1, 32))
    amax = np.abs(blocks).max(-1, keepdims=True)
    byte = np.maximum(np.where(amax > 0, np.frexp(amax)[1] - 1 + 127, 0) - down, 1)
    scale = np.exp2(byte - 127.0)
    codes = (blocks / scale).astype(np.float32).astype(dtype).astype(np.float64)
    return np.moveaxis((codes * scale).reshape(v.shape), -1, axis)


WIDE = False


def mx_kscale(k):
    if not WIDE:
        return np.ones(k)
    levels = np.array([10, -10, 5, -5, 0])
    if k % 512:
        return np.exp2(np.random.permutation(np.resize(levels, k // 32))).repeat(32)
    a = np.empty((k // 512, 16))
    for p in range(k // 512):
        a[p, :8] = np.random.permutation(np.resize(levels, 8))
        for g in range(8):
            far = levels[np.abs(levels - a[p, g]) >= 10]
            a[p, g + 8] = far[np.random.randint(len(far))]
    return np.exp2(a.ravel()).repeat(32)


def f64(x):
    return np.asarray(x).astype(np.float64)


def striped(idx):
    return np.tile(idx.reshape(-1, 16).T, (8, 1)).astype(np.uint16)


def unstriped(offs):
    return offs[:16].T.reshape(-1).astype(np.int64)


K, T, D, S, V, N = 1024, 1024, 4, 1024, 256, 128


def setup_inputs():
    n = np.random.standard_normal
    s = mx_kscale(K)[:, None]
    return {
        "xT": (n((K, T)) * s / np.sqrt(D)).astype(ml_dtypes.bfloat16).astype(np.float32),
        "w": (n((K, N)) / np.sqrt(K) / s).astype(np.float32),
        "offs": striped(np.concatenate([np.random.permutation(T)[:V] for _ in range(D)])),
    }


def reference(xT, w, offs):
    idx = unstriped(offs)
    x = sum(f64(xT)[:, idx[d * V:(d + 1) * V]] for d in range(D))
    return mxq(f64(w), 0, "e4m3").T @ mxq(x, 0, "e4m3")

@@ -1,0 +1,134 @@
+from contextlib import ExitStack
+
+import concourse.mybir as mybir
+
+K, T, D, V, M = 1024, 1024, 4, 256, 128
+FLOPS = 2 * K * V * M
+
+F32 = mybir.dt.float32
+BF16 = mybir.dt.bfloat16
+U32 = mybir.dt.uint32
+U16 = mybir.dt.uint16
+U8 = mybir.dt.uint8
+FP8X4 = mybir.dt.float8_e4m3fn_x4
+ADD = mybir.AluOpType.add
+
+P = 128
+PASSES = 2
+HALF = T // 2
+SPLIT = 704
+
+
+def tile_picked_hash_lin_none_sub_l_kernel(tc, xT, w, offs, out):
+    nc = tc.nc
+    adder = nc.gpsimd
+    with ExitStack() as ctx:
+        keep = ctx.enter_context(tc.tile_pool(name="keep", bufs=1))
+        psum = ctx.enter_context(tc.psum_pool(name="psum", bufs=1))
+
+        offsets = keep.tile([P, D * V // 16], U16, name="offsets")
+        rows = xT.rearrange("(g p u e) c -> g u p e c", g=PASSES, u=2, e=2)
+        raw = [[keep.tile([P, 2, HALF], F32, name=f"raw{j}_{h}") for h in range(2)] for j in range(4)]
+        w_raw = keep.tile([P, PASSES, 4, M], F32, name="w_raw")
+        for j in range(4):
+            for h in range(2):
+                nc.sync.dma_start(out=raw[j][h][:], in_=rows[j // 2, j % 2, :, :, h * HALF : (h + 1) * HALF])
+            if j == 0:
+                nc.sync.dma_start(offsets[:], offs)
+        nc.sync.dma_start(out=w_raw[:], in_=w.rearrange("(g p t) m -> p g t m", g=PASSES, t=4))
+
+        table = [keep.tile([P, T, 2], BF16, name=f"table{j}", align_bytes=64) for j in range(4)]
+        picked = [keep.tile([P, D, V, 2], BF16, name=f"picked{j}", align_bytes=64) for j in range(4)]
+        part = [keep.tile([P, 2, 2, V, 2], F32, name=f"part{g}", align_bytes=64) for g in range(PASSES)]
+        x_bf = [keep.tile([P, V, 2, 2], BF16, name=f"x_bf{g}", align_bytes=64) for g in range(PASSES)]
+        x_codes = keep.tile([P, PASSES, V], U32, name="x_codes", align_bytes=64)
+        x_scales = keep.tile([P, PASSES, V], U8, name="x_scales", align_bytes=64)
+        w_bf = keep.tile([P, PASSES, M, 4], BF16, name="w_bf", align_bytes=64)
+        w_codes = keep.tile([P, PASSES, M], U32, name="w_codes", align_bytes=64)
+        w_scales = keep.tile([P, PASSES, M], U8, name="w_scales", align_bytes=64)
+
+        def cast(copy, j, c0, c1):
+            h = c0 // HALF
+            src = raw[j][h][:, :, c0 - h * HALF : c1 - h * HALF]
+            copy(table[j][:, c0:c1, :], src.rearrange("p e c -> p c e"))
+
+        def gather(j, d0):
+            words = picked[j][:].rearrange("p d v e -> p (d v e)").bitcast(U32)
+            window = table[j][:].rearrange("p c e -> p (c e)").bitcast(U32)
+            lists = offsets[:, d0 * V // 16 : (d0 + 2) * V // 16]
+            nc.vector.tensor_copy(words[:, d0 * V : (d0 + 2) * V], window.indirect(lists))
+
+        def add_pair(eng, j, d0):
+            eng.tensor_tensor(part[j // 2][:, d0 // 2, j % 2], picked[j][:, d0], picked[j][:, d0 + 1], ADD)
+
+        def add_both(j):
+            pairs = picked[j][:].rearrange("p (a b) v e -> p b a (v e)", b=2)
+            dst = part[j // 2][:, :, j % 2].rearrange("p a v e -> p a (v e)")
+            nc.vector.tensor_tensor(dst, pairs[:, 0], pairs[:, 1], ADD)
+
+        def finish(g):
+            nc.vector.tensor_tensor(
+                x_bf[g][:],
+                part[g][:, 0].rearrange("p u v e -> p v u e"),
+                part[g][:, 1].rearrange("p u v e -> p v u e"),
+                ADD,
+            )
+
+        def quantize_x(g):
+            nc.vector.quantize_mx(
+                out=x_codes[:, g, :].bitcast(FP8X4),
+                scales=x_scales[:, g, :],
+                in_=x_bf[g][:].rearrange("p v u e -> p (v u e)"),
+            )
+
+        def quantize_w():
+            nc.vector.quantize_mx(
+                out=w_codes[:].rearrange("p g m -> p (g m)").bitcast(FP8X4),
+                scales=w_scales[:].rearrange("p g m -> p (g m)"),
+                in_=w_bf[:].rearrange("p g m t -> p (g m t)"),
+            )
+
+        cast(nc.scalar.copy, 0, 0, HALF)
+        cast(nc.scalar.copy, 0, HALF, SPLIT)
+        cast(nc.vector.tensor_copy, 0, SPLIT, T)
+        for j in range(1, 4):
+            cast(nc.scalar.copy, j, 0, HALF)
+            cast(nc.scalar.copy, j, HALF, T)
+        nc.scalar.copy(w_bf[:], w_raw[:].rearrange("p g t m -> p g m t"))
+
+        gather(0, 0)
+        add_pair(adder, 0, 0)
+        gather(0, 2)
+        add_pair(adder, 0, 2)
+        gather(1, 0)
+        add_pair(adder, 1, 0)
+        gather(1, 2)
+        add_pair(adder, 1, 2)
+        gather(2, 0)
+        add_pair(adder, 2, 0)
+        gather(2, 2)
+        finish(0)
+        add_pair(adder, 2, 2)
+        gather(3, 0)
+        add_pair(adder, 3, 0)
+        gather(3, 2)
+        add_pair(nc.vector, 3, 2)
+        quantize_x(0)
+        finish(1)
+        quantize_w()
+        quantize_x(1)
+
+        acc = psum.tile([M, V], F32, name="acc")
+        for g in range(PASSES):
+            nc.tensor.matmul_mx(
+                out=acc[:],
+                lhsT=w_codes[:, g, :].bitcast(FP8X4),
+                lhsT_scale=w_scales[:, g, :],
+                rhs=x_codes[:, g, :].bitcast(FP8X4),
+                rhs_scale=x_scales[:, g, :],
+                start=(g == 0),
+                stop=(g == PASSES - 1),
+            )
+        result = keep.tile([M, V], F32, name="result")
+        nc.vector.tensor_copy(result[:], acc[:])
+        nc.sync.dma_start(out=out, in_=result[:])

@@ -12,6 +12,7 @@ U16 = mybir.dt.uint16
 U8 = mybir.dt.uint8
 FP8X4 = mybir.dt.float8_e4m3fn_x4
 ADD = mybir.AluOpType.add
+COPY = mybir.ActivationFunctionType.Copy
 
 P = 128
 PASSES = 2
@@ -21,7 +22,7 @@ SPLIT = 704
 
 def tile_picked_hash_lin_none_sub_l_kernel(tc, xT, w, offs, out):
     nc = tc.nc
-    adder = nc.gpsimd
+    adder = nc.vector
     with ExitStack() as ctx:
         keep = ctx.enter_context(tc.tile_pool(name="keep", bufs=1))
         psum = ctx.enter_context(tc.psum_pool(name="psum", bufs=1))
@@ -37,7 +38,8 @@ def tile_picked_hash_lin_none_sub_l_kernel(tc, xT, w, offs, out):
                 nc.sync.dma_start(offsets[:], offs)
         nc.sync.dma_start(out=w_raw[:], in_=w.rearrange("(g p t) m -> p g t m", g=PASSES, t=4))
 
-        table = [keep.tile([P, T, 2], BF16, name=f"table{j}", align_bytes=64) for j in range(4)]
+        table = [keep.tile([P, T, 2], BF16, name=f"table{j}", align_bytes=64) for j in range(3)]
+        planes = keep.tile([P, 2, T], BF16, name="planes", align_bytes=64)
         picked = [keep.tile([P, D, V, 2], BF16, name=f"picked{j}", align_bytes=64) for j in range(4)]
         part = [keep.tile([P, 2, 2, V, 2], F32, name=f"part{g}", align_bytes=64) for g in range(PASSES)]
         x_bf = [keep.tile([P, V, 2, 2], BF16, name=f"x_bf{g}", align_bytes=64) for g in range(PASSES)]
@@ -57,6 +59,11 @@ def tile_picked_hash_lin_none_sub_l_kernel(tc, xT, w, offs, out):
             window = table[j][:].rearrange("p c e -> p (c e)").bitcast(U32)
             lists = offsets[:, d0 * V // 16 : (d0 + 2) * V // 16]
             nc.vector.tensor_copy(words[:, d0 * V : (d0 + 2) * V], window.indirect(lists))
+
+        def gather_planes(j, d):
+            lists = offsets[:, d * V // 16 : (d + 1) * V // 16]
+            for e in range(2):
+                nc.scalar.activation(picked[j][:, d, :, e], planes[:, e, :].indirect(lists), COPY)
 
         def add_pair(eng, j, d0):
             eng.tensor_tensor(part[j // 2][:, d0 // 2, j % 2], picked[j][:, d0], picked[j][:, d0 + 1], ADD)
@@ -91,29 +98,28 @@ def tile_picked_hash_lin_none_sub_l_kernel(tc, xT, w, offs, out):
         cast(nc.scalar.copy, 0, 0, HALF)
         cast(nc.scalar.copy, 0, HALF, SPLIT)
         cast(nc.vector.tensor_copy, 0, SPLIT, T)
-        for j in range(1, 4):
+        for j in range(1, 3):
             cast(nc.scalar.copy, j, 0, HALF)
             cast(nc.scalar.copy, j, HALF, T)
+        for h in range(2):
+            nc.scalar.copy(planes[:, :, h * HALF : (h + 1) * HALF], raw[3][h][:])
+        for d in range(D):
+            gather_planes(3, d)
         nc.scalar.copy(w_bf[:], w_raw[:].rearrange("p g t m -> p g m t"))
 
         gather(0, 0)
-        add_pair(adder, 0, 0)
         gather(0, 2)
-        add_pair(adder, 0, 2)
         gather(1, 0)
-        add_pair(adder, 1, 0)
+        add_both(0)
         gather(1, 2)
-        add_pair(adder, 1, 2)
         gather(2, 0)
-        add_pair(adder, 2, 0)
+        add_both(1)
         gather(2, 2)
         finish(0)
-        add_pair(adder, 2, 2)
-        gather(3, 0)
-        add_pair(adder, 3, 0)
-        gather(3, 2)
-        add_pair(nc.vector, 3, 2)
+        add_both(2)
         quantize_x(0)
+        add_pair(adder, 3, 0)
+        add_pair(adder, 3, 2)
         finish(1)
         quantize_w()
         quantize_x(1)

@@ -18,36 +18,45 @@ P = 128
 PASSES = 2
 HALF = T // 2
 SPLIT = 704
+VH = V // 2
 
 
 def tile_picked_hash_lin_none_sub_l_kernel(tc, xT, w, offs, out):
     nc = tc.nc
-    adder = nc.vector
     with ExitStack() as ctx:
         keep = ctx.enter_context(tc.tile_pool(name="keep", bufs=1))
         psum = ctx.enter_context(tc.psum_pool(name="psum", bufs=1))
 
         offsets = keep.tile([P, D * V // 16], U16, name="offsets")
         rows = xT.rearrange("(g p u e) c -> g u p e c", g=PASSES, u=2, e=2)
-        raw = [[keep.tile([P, 2, HALF], F32, name=f"raw{j}_{h}") for h in range(2)] for j in range(4)]
+        raw = [[keep.tile([P, 2, HALF], F32, name=f"raw{j}_{h}") for h in range(2)] for j in range(3)]
+        raw_planes = [keep.tile([P, T], F32, name=f"raw_plane{e}", align_bytes=64) for e in range(2)]
         w_raw = keep.tile([P, PASSES, 4, M], F32, name="w_raw")
-        for j in range(4):
+        for j in range(3):
             for h in range(2):
                 nc.sync.dma_start(out=raw[j][h][:], in_=rows[j // 2, j % 2, :, :, h * HALF : (h + 1) * HALF])
             if j == 0:
                 nc.sync.dma_start(offsets[:], offs)
+        for e in range(2):
+            nc.sync.dma_start(out=raw_planes[e][:], in_=rows[1, 1, :, e, :])
         nc.sync.dma_start(out=w_raw[:], in_=w.rearrange("(g p t) m -> p g t m", g=PASSES, t=4))
 
         table = [keep.tile([P, T, 2], BF16, name=f"table{j}", align_bytes=64) for j in range(3)]
-        planes = keep.tile([P, 2, T], BF16, name="planes", align_bytes=64)
-        picked = [keep.tile([P, D, V, 2], BF16, name=f"picked{j}", align_bytes=64) for j in range(4)]
-        part = [keep.tile([P, 2, 2, V, 2], F32, name=f"part{g}", align_bytes=64) for g in range(PASSES)]
-        x_bf = [keep.tile([P, V, 2, 2], BF16, name=f"x_bf{g}", align_bytes=64) for g in range(PASSES)]
-        x_codes = keep.tile([P, PASSES, V], U32, name="x_codes", align_bytes=64)
+        planes = [keep.tile([P, T], BF16, name=f"plane{e}", align_bytes=64) for e in range(2)]
+        picked = [[keep.tile([P, 2, V, 2], BF16, name=f"picked{j}_{a}", align_bytes=64) for a in range(2)] for j in range(4)]
+        part = {(g, a): keep.tile([P, 2, V, 2], F32, name=f"part{g}_{a}", align_bytes=64) for g, a in ((0, 0), (0, 1), (1, 0))}
+        x_bf0 = keep.tile([P, V, 2, 2], BF16, name="x_bf0", align_bytes=64)
+        x_bf1 = {0: keep.tile([P, VH, 2, 2], BF16, name="x_bf1_0", align_bytes=64)}
+        x_codes = {1: keep.tile([P, V], U32, name="x_codes1", align_bytes=64)}
         x_scales = keep.tile([P, PASSES, V], U8, name="x_scales", align_bytes=64)
         w_bf = keep.tile([P, PASSES, M, 4], BF16, name="w_bf", align_bytes=64)
         w_codes = keep.tile([P, PASSES, M], U32, name="w_codes", align_bytes=64)
         w_scales = keep.tile([P, PASSES, M], U8, name="w_scales", align_bytes=64)
+        acc = [psum.tile([M, VH], F32, name=f"acc{h}") for h in range(2)]
+        result = [keep.tile([M, VH], F32, name=f"result{h}") for h in range(2)]
+
+        def entries(first, count):
+            return offsets[:, first // 16 : (first + count) // 16]
 
         def cast(copy, j, c0, c1):
             h = c0 // HALF
@@ -55,44 +64,64 @@ def tile_picked_hash_lin_none_sub_l_kernel(tc, xT, w, offs, out):
             copy(table[j][:, c0:c1, :], src.rearrange("p e c -> p c e"))
 
         def gather(j, d0):
-            words = picked[j][:].rearrange("p d v e -> p (d v e)").bitcast(U32)
+            words = picked[j][d0 // 2][:].rearrange("p d v e -> p (d v e)").bitcast(U32)
             window = table[j][:].rearrange("p c e -> p (c e)").bitcast(U32)
-            lists = offsets[:, d0 * V // 16 : (d0 + 2) * V // 16]
-            nc.vector.tensor_copy(words[:, d0 * V : (d0 + 2) * V], window.indirect(lists))
+            nc.vector.tensor_copy(words, window.indirect(entries(d0 * V, 2 * V)))
 
-        def gather_planes(j, d):
-            lists = offsets[:, d * V // 16 : (d + 1) * V // 16]
+        def gather_scalar(d, v0, v1):
             for e in range(2):
-                nc.scalar.activation(picked[j][:, d, :, e], planes[:, e, :].indirect(lists), COPY)
+                window = planes[e][:].indirect(entries(d * V + v0, v1 - v0))
+                nc.scalar.activation(picked[3][d // 2][:, d % 2, v0:v1, e], window, COPY)
 
-        def add_pair(eng, j, d0):
-            eng.tensor_tensor(part[j // 2][:, d0 // 2, j % 2], picked[j][:, d0], picked[j][:, d0 + 1], ADD)
+        def gather_vector(d, v0, v1):
+            for e in range(2):
+                window = raw_planes[e][:].indirect(entries(d * V + v0, v1 - v0))
+                nc.vector.tensor_copy(picked[3][d // 2][:, d % 2, v0:v1, e], window)
 
-        def add_both(j):
-            pairs = picked[j][:].rearrange("p (a b) v e -> p b a (v e)", b=2)
-            dst = part[j // 2][:, :, j % 2].rearrange("p a v e -> p a (v e)")
-            nc.vector.tensor_tensor(dst, pairs[:, 0], pairs[:, 1], ADD)
+        def add_pair(eng, j, d0, v0=0, v1=V):
+            eng.tensor_tensor(
+                part[j // 2, d0 // 2][:, j % 2, v0:v1], picked[j][d0 // 2][:, 0, v0:v1], picked[j][d0 // 2][:, 1, v0:v1], ADD
+            )
 
-        def finish(g):
+        def finish(h):
+            ids = slice(h * VH, (h + 1) * VH)
             nc.vector.tensor_tensor(
-                x_bf[g][:],
-                part[g][:, 0].rearrange("p u v e -> p v u e"),
-                part[g][:, 1].rearrange("p u v e -> p v u e"),
+                x_bf1[h][:],
+                part[1, 0][:, :, ids].rearrange("p u v e -> p v u e"),
+                part[1, 1][:, :, ids].rearrange("p u v e -> p v u e"),
                 ADD,
             )
 
-        def quantize_x(g):
+        def finish_pair(g, u):
+            nc.gpsimd.tensor_tensor(x_bf0[:, :, u, :], part[g, 0][:, u], part[g, 1][:, u], ADD)
+
+        def quantize_x(g, v0, v1, src):
             nc.vector.quantize_mx(
-                out=x_codes[:, g, :].bitcast(FP8X4),
-                scales=x_scales[:, g, :],
-                in_=x_bf[g][:].rearrange("p v u e -> p (v u e)"),
+                out=x_codes[g][:, v0:v1].bitcast(FP8X4),
+                scales=x_scales[:, g, v0:v1],
+                in_=src[:].rearrange("p v u e -> p (v u e)"),
             )
 
-        def quantize_w():
+        def cast_w(g):
+            nc.scalar.copy(w_bf[:, g], w_raw[:, g].rearrange("p t m -> p m t"))
+
+        def quantize_w(g):
             nc.vector.quantize_mx(
-                out=w_codes[:].rearrange("p g m -> p (g m)").bitcast(FP8X4),
-                scales=w_scales[:].rearrange("p g m -> p (g m)"),
-                in_=w_bf[:].rearrange("p g m t -> p (g m t)"),
+                out=w_codes[:, g, :].bitcast(FP8X4),
+                scales=w_scales[:, g, :],
+                in_=w_bf[:, g].rearrange("p m t -> p (m t)"),
+            )
+
+        def multiply(g, h):
+            ids = slice(h * VH, (h + 1) * VH)
+            nc.tensor.matmul_mx(
+                out=acc[h][:],
+                lhsT=w_codes[:, g, :].bitcast(FP8X4),
+                lhsT_scale=w_scales[:, g, :],
+                rhs=x_codes[g][:, ids].bitcast(FP8X4),
+                rhs_scale=x_scales[:, g, ids],
+                start=(g == 0),
+                stop=(g == PASSES - 1),
             )
 
         cast(nc.scalar.copy, 0, 0, HALF)
@@ -101,40 +130,46 @@ def tile_picked_hash_lin_none_sub_l_kernel(tc, xT, w, offs, out):
         for j in range(1, 3):
             cast(nc.scalar.copy, j, 0, HALF)
             cast(nc.scalar.copy, j, HALF, T)
-        for h in range(2):
-            nc.scalar.copy(planes[:, :, h * HALF : (h + 1) * HALF], raw[3][h][:])
-        for d in range(D):
-            gather_planes(3, d)
-        nc.scalar.copy(w_bf[:], w_raw[:].rearrange("p g t m -> p g m t"))
+        for e in range(2):
+            nc.scalar.copy(planes[e][:], raw_planes[e][:])
+        gather_scalar(0, 0, V)
+        gather_scalar(1, 0, V)
+        cast_w(0)
+        gather_scalar(2, 0, VH)
+        cast_w(1)
 
         gather(0, 0)
+        add_pair(nc.gpsimd, 0, 0)
         gather(0, 2)
-        gather(1, 0)
-        add_both(0)
-        gather(1, 2)
+        add_pair(nc.vector, 0, 2)
+        finish_pair(0, 0)
+        for d0 in (0, 2):
+            gather(1, d0)
+            add_pair(nc.gpsimd, 1, d0)
+        finish_pair(0, 1)
         gather(2, 0)
-        add_both(1)
+        add_pair(nc.gpsimd, 2, 0)
         gather(2, 2)
-        finish(0)
-        add_both(2)
-        quantize_x(0)
-        add_pair(adder, 3, 0)
-        add_pair(adder, 3, 2)
+        gather_vector(2, VH, V)
+        gather_vector(3, 0, V)
+        part[1, 1] = keep.tile([P, 2, V, 2], F32, name="part1_1", tag="raw_plane1", align_bytes=64)
+        x_codes[0] = keep.tile([P, V], U32, name="x_codes0", tag="raw_plane0", align_bytes=64)
+        add_pair(nc.vector, 2, 2)
+        add_pair(nc.vector, 3, 2, VH, V)
+        add_pair(nc.vector, 3, 0)
+        quantize_x(0, 0, V, x_bf0)
+        quantize_w(0)
+        add_pair(nc.vector, 3, 2, 0, VH)
+        x_bf1[1] = keep.tile([P, VH, 2, 2], BF16, name="x_bf1_1", tag="plane1", align_bytes=64)
         finish(1)
-        quantize_w()
-        quantize_x(1)
-
-        acc = psum.tile([M, V], F32, name="acc")
+        quantize_w(1)
+        finish(0)
+        quantize_x(1, VH, V, x_bf1[1])
+        quantize_x(1, 0, VH, x_bf1[0])
         for g in range(PASSES):
-            nc.tensor.matmul_mx(
-                out=acc[:],
-                lhsT=w_codes[:, g, :].bitcast(FP8X4),
-                lhsT_scale=w_scales[:, g, :],
-                rhs=x_codes[:, g, :].bitcast(FP8X4),
-                rhs_scale=x_scales[:, g, :],
-                start=(g == 0),
-                stop=(g == PASSES - 1),
-            )
-        result = keep.tile([M, V], F32, name="result")
-        nc.vector.tensor_copy(result[:], acc[:])
-        nc.sync.dma_start(out=out, in_=result[:])
+            for h in (1, 0):
+                multiply(g, h)
+        nc.scalar.copy(result[1][:], acc[1][:])
+        nc.vector.tensor_copy(result[0][:], acc[0][:])
+        for h in (1, 0):
+            nc.sync.dma_start(out=out[:, h * VH : (h + 1) * VH], in_=result[h][:])

@@ -1,6 +1,7 @@
 from contextlib import ExitStack
 
 import concourse.mybir as mybir
+from concourse.masks import make_identity
 
 K, T, D, V, M = 1024, 1024, 4, 256, 128
 FLOPS = 2 * K * V * M
@@ -12,12 +13,10 @@ U16 = mybir.dt.uint16
 U8 = mybir.dt.uint8
 FP8X4 = mybir.dt.float8_e4m3fn_x4
 ADD = mybir.AluOpType.add
-COPY = mybir.ActivationFunctionType.Copy
 
 P = 128
 PASSES = 2
 HALF = T // 2
-SPLIT = 704
 VH = V // 2
 
 
@@ -29,28 +28,27 @@ def tile_picked_hash_lin_none_sub_l_kernel(tc, xT, w, offs, out):
 
         offsets = keep.tile([P, D * V // 16], U16, name="offsets")
         rows = xT.rearrange("(g p u e) c -> g u p e c", g=PASSES, u=2, e=2)
-        raw = [[keep.tile([P, 2, HALF], F32, name=f"raw{j}_{h}") for h in range(2)] for j in range(3)]
-        raw_planes = [keep.tile([P, T], F32, name=f"raw_plane{e}", align_bytes=64) for e in range(2)]
+        pair = [keep.tile([P, 2, T], F32, name=f"pair{j}", align_bytes=64) for j in range(4)]
         w_raw = keep.tile([P, PASSES, 4, M], F32, name="w_raw")
-        for j in range(3):
+        for j in range(4):
             for h in range(2):
-                nc.sync.dma_start(out=raw[j][h][:], in_=rows[j // 2, j % 2, :, :, h * HALF : (h + 1) * HALF])
+                cols = slice(h * HALF, (h + 1) * HALF)
+                nc.sync.dma_start(out=pair[j][:, :, cols], in_=rows[j // 2, j % 2, :, :, cols])
             if j == 0:
                 nc.sync.dma_start(offsets[:], offs)
-        for e in range(2):
-            nc.sync.dma_start(out=raw_planes[e][:], in_=rows[1, 1, :, e, :])
         nc.sync.dma_start(out=w_raw[:], in_=w.rearrange("(g p t) m -> p g t m", g=PASSES, t=4))
 
-        table = [keep.tile([P, T, 2], BF16, name=f"table{j}", align_bytes=64) for j in range(3)]
-        planes = [keep.tile([P, T], BF16, name=f"plane{e}", align_bytes=64) for e in range(2)]
-        picked = [[keep.tile([P, 2, V, 2], BF16, name=f"picked{j}_{a}", align_bytes=64) for a in range(2)] for j in range(4)]
-        part = {(g, a): keep.tile([P, 2, V, 2], F32, name=f"part{g}_{a}", align_bytes=64) for g, a in ((0, 0), (0, 1), (1, 0))}
+        ident = keep.tile([P, P], F32, name="ident")
+        make_identity(nc, ident[:])
+
+        picked = {(j, a): keep.tile([P, 2, V, 2], BF16, name=f"picked{j}_{a}", align_bytes=64) for j in range(4) for a in range(2)}
+        part = {(j, a): keep.tile([P, 2, V], F32, name=f"part{j}_{a}", align_bytes=64) for j in range(2) for a in range(2)}
+        part23 = keep.tile([P, 2, 2, V, 2], F32, name="part23", align_bytes=64)
+        turned = [psum.tile([P, 2, 2, P], F32, name=f"turned{u}") for u in range(2)]
         x_bf0 = keep.tile([P, V, 2, 2], BF16, name="x_bf0", align_bytes=64)
-        x_bf1 = {0: keep.tile([P, VH, 2, 2], BF16, name="x_bf1_0", align_bytes=64)}
+        x_bf1 = [keep.tile([P, VH, 2, 2], BF16, name=f"x_bf1_{h}", align_bytes=64) for h in range(2)]
         x_codes = {1: keep.tile([P, V], U32, name="x_codes1", align_bytes=64)}
         x_scales = keep.tile([P, PASSES, V], U8, name="x_scales", align_bytes=64)
-        w_bf = keep.tile([P, PASSES, M, 4], BF16, name="w_bf", align_bytes=64)
-        w_codes = keep.tile([P, PASSES, M], U32, name="w_codes", align_bytes=64)
         w_scales = keep.tile([P, PASSES, M], U8, name="w_scales", align_bytes=64)
         acc = [psum.tile([M, VH], F32, name=f"acc{h}") for h in range(2)]
         result = [keep.tile([M, VH], F32, name=f"result{h}") for h in range(2)]
@@ -58,42 +56,35 @@ def tile_picked_hash_lin_none_sub_l_kernel(tc, xT, w, offs, out):
         def entries(first, count):
             return offsets[:, first // 16 : (first + count) // 16]
 
-        def cast(copy, j, c0, c1):
-            h = c0 // HALF
-            src = raw[j][h][:, :, c0 - h * HALF : c1 - h * HALF]
-            copy(table[j][:, c0:c1, :], src.rearrange("p e c -> p c e"))
+        def fill(copy, j, c0, c1):
+            halves = pair[j][:, 1].bitcast(BF16).rearrange("p (c e) -> p c e", e=2)
+            copy(halves[:, c0:c1, 0], pair[j][:, 0, c0:c1])
 
-        def gather(j, d0):
-            words = picked[j][d0 // 2][:].rearrange("p d v e -> p (d v e)").bitcast(U32)
-            window = table[j][:].rearrange("p c e -> p (c e)").bitcast(U32)
-            nc.vector.tensor_copy(words, window.indirect(entries(d0 * V, 2 * V)))
+        def gather(j, a):
+            words = picked[j, a][:].rearrange("p d v e -> p (d v e)").bitcast(U32)
+            nc.vector.tensor_copy(words, pair[j][:, 1].bitcast(U32).indirect(entries(2 * a * V, 2 * V)))
 
-        def gather_scalar(d, v0, v1):
-            for e in range(2):
-                window = planes[e][:].indirect(entries(d * V + v0, v1 - v0))
-                nc.scalar.activation(picked[3][d // 2][:, d % 2, v0:v1, e], window, COPY)
+        def turn_and_add(u, e, terms):
+            for h in range(2):
+                for i, term in enumerate(terms):
+                    nc.tensor.matmul(
+                        turned[u][:, h, e, :], term[:, h * VH : (h + 1) * VH], ident[:],
+                        is_transpose=True, start=(i == 0), stop=(i == len(terms) - 1),
+                    )
 
-        def gather_vector(d, v0, v1):
-            for e in range(2):
-                window = raw_planes[e][:].indirect(entries(d * V + v0, v1 - v0))
-                nc.vector.tensor_copy(picked[3][d // 2][:, d % 2, v0:v1, e], window)
-
-        def add_pair(eng, j, d0, v0=0, v1=V):
-            eng.tensor_tensor(
-                part[j // 2, d0 // 2][:, j % 2, v0:v1], picked[j][d0 // 2][:, 0, v0:v1], picked[j][d0 // 2][:, 1, v0:v1], ADD
-            )
+        def turn_back(u):
+            for h in range(2):
+                words = rounded[u][:, h].rearrange("v p e -> v (p e)").bitcast(F32)
+                nc.tensor.transpose(back[:, u, h * VH : (h + 1) * VH], words, ident[:])
 
         def finish(h):
             ids = slice(h * VH, (h + 1) * VH)
             nc.vector.tensor_tensor(
                 x_bf1[h][:],
-                part[1, 0][:, :, ids].rearrange("p u v e -> p v u e"),
-                part[1, 1][:, :, ids].rearrange("p u v e -> p v u e"),
+                part23[:, :, 0, ids].rearrange("p u v e -> p v u e"),
+                part23[:, :, 1, ids].rearrange("p u v e -> p v u e"),
                 ADD,
             )
-
-        def finish_pair(g, u):
-            nc.gpsimd.tensor_tensor(x_bf0[:, :, u, :], part[g, 0][:, u], part[g, 1][:, u], ADD)
 
         def quantize_x(g, v0, v1, src):
             nc.vector.quantize_mx(
@@ -102,17 +93,7 @@ def tile_picked_hash_lin_none_sub_l_kernel(tc, xT, w, offs, out):
                 in_=src[:].rearrange("p v u e -> p (v u e)"),
             )
 
-        def cast_w(g):
-            nc.scalar.copy(w_bf[:, g], w_raw[:, g].rearrange("p t m -> p m t"))
-
-        def quantize_w(g):
-            nc.vector.quantize_mx(
-                out=w_codes[:, g, :].bitcast(FP8X4),
-                scales=w_scales[:, g, :],
-                in_=w_bf[:, g].rearrange("p m t -> p (m t)"),
-            )
-
-        def multiply(g, h):
+        def multiply(g, h, first):
             ids = slice(h * VH, (h + 1) * VH)
             nc.tensor.matmul_mx(
                 out=acc[h][:],
@@ -120,55 +101,61 @@ def tile_picked_hash_lin_none_sub_l_kernel(tc, xT, w, offs, out):
                 lhsT_scale=w_scales[:, g, :],
                 rhs=x_codes[g][:, ids].bitcast(FP8X4),
                 rhs_scale=x_scales[:, g, ids],
-                start=(g == 0),
-                stop=(g == PASSES - 1),
+                start=first,
+                stop=not first,
             )
 
-        cast(nc.scalar.copy, 0, 0, HALF)
-        cast(nc.scalar.copy, 0, HALF, SPLIT)
-        cast(nc.vector.tensor_copy, 0, SPLIT, T)
-        for j in range(1, 3):
-            cast(nc.scalar.copy, j, 0, HALF)
-            cast(nc.scalar.copy, j, HALF, T)
-        for e in range(2):
-            nc.scalar.copy(planes[e][:], raw_planes[e][:])
-        gather_scalar(0, 0, V)
-        gather_scalar(1, 0, V)
-        cast_w(0)
-        gather_scalar(2, 0, VH)
-        cast_w(1)
-
-        gather(0, 0)
-        add_pair(nc.gpsimd, 0, 0)
-        gather(0, 2)
-        add_pair(nc.vector, 0, 2)
-        finish_pair(0, 0)
-        for d0 in (0, 2):
-            gather(1, d0)
-            add_pair(nc.gpsimd, 1, d0)
-        finish_pair(0, 1)
-        gather(2, 0)
-        add_pair(nc.gpsimd, 2, 0)
-        gather(2, 2)
-        gather_vector(2, VH, V)
-        gather_vector(3, 0, V)
-        part[1, 1] = keep.tile([P, 2, V, 2], F32, name="part1_1", tag="raw_plane1", align_bytes=64)
-        x_codes[0] = keep.tile([P, V], U32, name="x_codes0", tag="raw_plane0", align_bytes=64)
-        add_pair(nc.vector, 2, 2)
-        add_pair(nc.vector, 3, 2, VH, V)
-        add_pair(nc.vector, 3, 0)
-        quantize_x(0, 0, V, x_bf0)
-        quantize_w(0)
-        add_pair(nc.vector, 3, 2, 0, VH)
-        x_bf1[1] = keep.tile([P, VH, 2, 2], BF16, name="x_bf1_1", tag="plane1", align_bytes=64)
+        fill(nc.scalar.copy, 0, 0, HALF)
+        fill(nc.vector.tensor_copy, 0, HALF, T)
+        for j in (1, 2, 3):
+            for h in range(2):
+                fill(nc.scalar.copy, j, h * HALF, (h + 1) * HALF)
+        for j in range(2):
+            for a in range(2):
+                gather(j, a)
+                nc.gpsimd.tensor_tensor(
+                    part[j, a][:],
+                    picked[j, a][:, 0].rearrange("p v e -> p e v"),
+                    picked[j, a][:, 1].rearrange("p v e -> p e v"),
+                    ADD,
+                )
+        for a in range(2):
+            gather(2, a)
+            nc.gpsimd.tensor_tensor(part23[:, 0, a], picked[2, a][:, 0], picked[2, a][:, 1], ADD)
+        for a in range(2):
+            gather(3, a)
+        spent = pair[3][:, 0, HALF:T].bitcast(BF16).rearrange("v (u h p e) -> v u h p e", u=2, h=2, e=2)
+        rounded = [spent[:, u] for u in range(2)]
+        w_bf = keep.tile([P, PASSES, M, 4], BF16, name="w_bf", align_bytes=64)
+        for u in range(2):
+            for e in range(2):
+                turn_and_add(u, e, [part[u, a][:, e] for a in range(2)])
+            nc.scalar.copy(rounded[u], turned[u][:].rearrange("v h e p -> v h p e"))
+        back = psum.tile([P, 2, V], F32, name="back", tag="turned1")
+        for u in range(2):
+            turn_back(u)
+        nc.scalar.copy(w_bf[:], w_raw[:].rearrange("p g t m -> p g m t"))
+        nc.scalar.copy(
+            x_bf0[:].rearrange("p v u e -> p (v u e)").bitcast(F32).rearrange("p (v u) -> p v u", u=2),
+            back[:].rearrange("p u v -> p v u"),
+        )
+        for a in range(2):
+            nc.vector.tensor_tensor(part23[:, 1, a], picked[3, a][:, 0], picked[3, a][:, 1], ADD)
+        w_codes = keep.tile([P, PASSES, M], U32, name="w_codes", tag="pair3", align_bytes=64)
+        nc.vector.quantize_mx(
+            out=w_codes[:].rearrange("p g m -> p (g m)").bitcast(FP8X4),
+            scales=w_scales[:].rearrange("p g m -> p (g m)"),
+            in_=w_bf[:].rearrange("p g m t -> p (g m t)"),
+        )
         finish(1)
-        quantize_w(1)
         finish(0)
         quantize_x(1, VH, V, x_bf1[1])
+        x_codes[0] = keep.tile([P, V], U32, name="x_codes0", tag="part23", align_bytes=64)
+        quantize_x(0, 0, V, x_bf0)
         quantize_x(1, 0, VH, x_bf1[0])
-        for g in range(PASSES):
-            for h in (1, 0):
-                multiply(g, h)
+        for h in (1, 0):
+            multiply(h, h, True)
+            multiply(1 - h, h, False)
         nc.scalar.copy(result[1][:], acc[1][:])
         nc.vector.tensor_copy(result[0][:], acc[0][:])
         for h in (1, 0):

@@ -18,6 +18,8 @@ P = 128
 PASSES = 2
 HALF = T // 2
 VH = V // 2
+CUT = 576
+PIECES = ((0, CUT), (CUT, T))
 
 
 def tile_picked_hash_lin_none_sub_l_kernel(tc, xT, w, offs, out):
@@ -31,8 +33,8 @@ def tile_picked_hash_lin_none_sub_l_kernel(tc, xT, w, offs, out):
         pair = [keep.tile([P, 2, T], F32, name=f"pair{j}", align_bytes=64) for j in range(4)]
         w_raw = keep.tile([P, PASSES, 4, M], F32, name="w_raw")
         for j in range(4):
-            for h in range(2):
-                cols = slice(h * HALF, (h + 1) * HALF)
+            for c0, c1 in PIECES:
+                cols = slice(c0, c1)
                 nc.sync.dma_start(out=pair[j][:, :, cols], in_=rows[j // 2, j % 2, :, :, cols])
             if j == 0:
                 nc.sync.dma_start(offsets[:], offs)
@@ -105,11 +107,11 @@ def tile_picked_hash_lin_none_sub_l_kernel(tc, xT, w, offs, out):
                 stop=not first,
             )
 
-        fill(nc.scalar.copy, 0, 0, HALF)
-        fill(nc.vector.tensor_copy, 0, HALF, T)
+        fill(nc.scalar.copy, 0, 0, CUT)
+        fill(nc.vector.tensor_copy, 0, CUT, T)
         for j in (1, 2, 3):
-            for h in range(2):
-                fill(nc.scalar.copy, j, h * HALF, (h + 1) * HALF)
+            for c0, c1 in PIECES:
+                fill(nc.scalar.copy, j, c0, c1)
         for j in range(2):
             for a in range(2):
                 gather(j, a)
@@ -126,26 +128,26 @@ def tile_picked_hash_lin_none_sub_l_kernel(tc, xT, w, offs, out):
             gather(3, a)
         spent = pair[3][:, 0, HALF:T].bitcast(BF16).rearrange("v (u h p e) -> v u h p e", u=2, h=2, e=2)
         rounded = [spent[:, u] for u in range(2)]
-        w_bf = keep.tile([P, PASSES, M, 4], BF16, name="w_bf", align_bytes=64)
+        w_bf = pair[3][:, 0, 0:HALF].bitcast(BF16).rearrange("p (g m t) -> p g m t", g=PASSES, t=4)
         for u in range(2):
             for e in range(2):
                 turn_and_add(u, e, [part[u, a][:, e] for a in range(2)])
             nc.scalar.copy(rounded[u], turned[u][:].rearrange("v h e p -> v h p e"))
-        back = psum.tile([P, 2, V], F32, name="back", tag="turned1")
+        back = psum.tile([P, 2, V], F32, name="back")
         for u in range(2):
             turn_back(u)
-        nc.scalar.copy(w_bf[:], w_raw[:].rearrange("p g t m -> p g m t"))
+        nc.scalar.copy(w_bf, w_raw[:].rearrange("p g t m -> p g m t"))
         nc.scalar.copy(
             x_bf0[:].rearrange("p v u e -> p (v u e)").bitcast(F32).rearrange("p (v u) -> p v u", u=2),
             back[:].rearrange("p u v -> p v u"),
         )
         for a in range(2):
             nc.vector.tensor_tensor(part23[:, 1, a], picked[3, a][:, 0], picked[3, a][:, 1], ADD)
-        w_codes = keep.tile([P, PASSES, M], U32, name="w_codes", tag="pair3", align_bytes=64)
+        w_codes = keep.tile([P, PASSES, M], U32, name="w_codes", tag="picked3_0", align_bytes=64)
         nc.vector.quantize_mx(
             out=w_codes[:].rearrange("p g m -> p (g m)").bitcast(FP8X4),
             scales=w_scales[:].rearrange("p g m -> p (g m)"),
-            in_=w_bf[:].rearrange("p g m t -> p (g m t)"),
+            in_=w_bf.rearrange("p g m t -> p (g m t)"),
         )
         finish(1)
         finish(0)

@@ -92,7 +92,7 @@ def tile_picked_hash_lin_none_sub_l_kernel(tc, xT, w, offs, out):
             nc.vector.quantize_mx(
                 out=x_codes[g][:, v0:v1].bitcast(FP8X4),
                 scales=x_scales[:, g, v0:v1],
-                in_=src[:].rearrange("p v u e -> p (v u e)"),
+                in_=src.rearrange("p v u e -> p (v u e)"),
             )
 
         def multiply(g, h, first):
@@ -151,13 +151,14 @@ def tile_picked_hash_lin_none_sub_l_kernel(tc, xT, w, offs, out):
         )
         finish(1)
         finish(0)
-        quantize_x(1, VH, V, x_bf1[1])
+        quantize_x(1, VH, V, x_bf1[1][:])
         x_codes[0] = keep.tile([P, V], U32, name="x_codes0", tag="part23", align_bytes=64)
-        quantize_x(0, 0, V, x_bf0)
-        quantize_x(1, 0, VH, x_bf1[0])
+        quantize_x(0, VH, V, x_bf0[:, VH:V])
+        quantize_x(1, 0, VH, x_bf1[0][:])
+        quantize_x(0, 0, VH, x_bf0[:, 0:VH])
         for h in (1, 0):
-            multiply(h, h, True)
-            multiply(1 - h, h, False)
+            multiply(1, h, True)
+            multiply(0, h, False)
         nc.scalar.copy(result[1][:], acc[1][:])
         nc.vector.tensor_copy(result[0][:], acc[0][:])
         for h in (1, 0):

@@ -13,6 +13,7 @@ U16 = mybir.dt.uint16
 U8 = mybir.dt.uint8
 FP8X4 = mybir.dt.float8_e4m3fn_x4
 ADD = mybir.AluOpType.add
+COPY = mybir.ActivationFunctionType.Copy
 
 P = 128
 PASSES = 2
@@ -20,36 +21,43 @@ HALF = T // 2
 VH = V // 2
 CUT = 576
 PIECES = ((0, CUT), (CUT, T))
+PAIR_ROWS = ((0, 0), (1, 0), (1, 1))
 
 
 def tile_picked_hash_lin_none_sub_l_kernel(tc, xT, w, offs, out):
     nc = tc.nc
     with ExitStack() as ctx:
         keep = ctx.enter_context(tc.tile_pool(name="keep", bufs=1))
+        ring = ctx.enter_context(tc.tile_pool(name="ring", bufs=1))
         psum = ctx.enter_context(tc.psum_pool(name="psum", bufs=1))
 
         offsets = keep.tile([P, D * V // 16], U16, name="offsets")
         rows = xT.rearrange("(g p u e) c -> g u p e c", g=PASSES, u=2, e=2)
-        pair = [keep.tile([P, 2, T], F32, name=f"pair{j}", align_bytes=64) for j in range(4)]
+        pair = [keep.tile([P, 2, T], F32, name=f"pair{j}", align_bytes=64) for j in range(3)]
+        single = [keep.tile([P, T], F32, name=f"single{e}", align_bytes=64) for e in range(2)]
         w_raw = keep.tile([P, PASSES, 4, M], F32, name="w_raw")
-        for j in range(4):
+        for j in range(3):
             for c0, c1 in PIECES:
                 cols = slice(c0, c1)
-                nc.sync.dma_start(out=pair[j][:, :, cols], in_=rows[j // 2, j % 2, :, :, cols])
+                nc.sync.dma_start(out=pair[j][:, :, cols], in_=rows[PAIR_ROWS[j][0], PAIR_ROWS[j][1], :, :, cols])
             if j == 0:
                 nc.sync.dma_start(offsets[:], offs)
+            if j < 2:
+                nc.sync.dma_start(out=single[j][:], in_=rows[0, 1, :, j, :])
         nc.sync.dma_start(out=w_raw[:], in_=w.rearrange("(g p t) m -> p g t m", g=PASSES, t=4))
 
         ident = keep.tile([P, P], F32, name="ident")
         make_identity(nc, ident[:])
 
-        picked = {(j, a): keep.tile([P, 2, V, 2], BF16, name=f"picked{j}_{a}", align_bytes=64) for j in range(4) for a in range(2)}
-        part = {(j, a): keep.tile([P, 2, V], F32, name=f"part{j}_{a}", align_bytes=64) for j in range(2) for a in range(2)}
-        part23 = keep.tile([P, 2, 2, V, 2], F32, name="part23", align_bytes=64)
-        turned = [psum.tile([P, 2, 2, P], F32, name=f"turned{u}") for u in range(2)]
+        def at(shape, dtype, name, slot, skip=0):
+            return ring.tile(shape, dtype, name=name, offset=2048 * slot + skip, align_bytes=64)
+
+        picked = {(j, a): at([P, 2, V, 2], BF16, f"picked{j}_{a}", 2 * j + a) for j in range(3) for a in range(2)}
+        part = {(j, a): at([P, 2, V], F32, f"part{j}_{a}", 6 + 2 * j + a) for j in range(1) for a in range(2)}
+        part12 = keep.tile([P, 2, 2, V, 2], F32, name="part12", align_bytes=64)
+        turned = [psum.tile([P, 2, 2, P], F32, name=f"turned_h{h}") for h in range(2)]
         x_bf0 = keep.tile([P, V, 2, 2], BF16, name="x_bf0", align_bytes=64)
         x_bf1 = [keep.tile([P, VH, 2, 2], BF16, name=f"x_bf1_{h}", align_bytes=64) for h in range(2)]
-        x_codes = {1: keep.tile([P, V], U32, name="x_codes1", align_bytes=64)}
         x_scales = keep.tile([P, PASSES, V], U8, name="x_scales", align_bytes=64)
         w_scales = keep.tile([P, PASSES, M], U8, name="w_scales", align_bytes=64)
         acc = [psum.tile([M, VH], F32, name=f"acc{h}") for h in range(2)]
@@ -66,27 +74,43 @@ def tile_picked_hash_lin_none_sub_l_kernel(tc, xT, w, offs, out):
             words = picked[j, a][:].rearrange("p d v e -> p (d v e)").bitcast(U32)
             nc.vector.tensor_copy(words, pair[j][:, 1].bitcast(U32).indirect(entries(2 * a * V, 2 * V)))
 
-        def turn_and_add(u, e, terms):
-            for h in range(2):
-                for i, term in enumerate(terms):
-                    nc.tensor.matmul(
-                        turned[u][:, h, e, :], term[:, h * VH : (h + 1) * VH], ident[:],
-                        is_transpose=True, start=(i == 0), stop=(i == len(terms) - 1),
-                    )
+        done = []
 
-        def turn_back(u):
-            for h in range(2):
-                words = rounded[u][:, h].rearrange("v p e -> v (p e)").bitcast(F32)
-                nc.tensor.transpose(back[:, u, h * VH : (h + 1) * VH], words, ident[:])
+        def turn_half(h, u, e, term):
+            nc.tensor.matmul(
+                turned[h][:, u, e, :], term, ident[:],
+                is_transpose=True, start=(done.count(h) == 0), stop=(done.count(h) == 2 * D + 3),
+            )
+            done.append(h)
 
-        def finish(h):
-            ids = slice(h * VH, (h + 1) * VH)
-            nc.vector.tensor_tensor(
-                x_bf1[h][:],
-                part23[:, :, 0, ids].rearrange("p u v e -> p v u e"),
-                part23[:, :, 1, ids].rearrange("p u v e -> p v u e"),
+        def gather_single(e, on_scalar, r0, got):
+            n = got.shape[1] // VH
+            window = single[e][:].indirect(entries(r0 * VH, n * VH))
+            if on_scalar:
+                nc.scalar.activation(got[:, :], window, COPY)
+            else:
+                nc.vector.tensor_copy(got[:, :], window)
+            for r in range(n):
+                turn_half((r0 + r) % 2, 1, e, got[:, r * VH : (r + 1) * VH])
+
+        def turn_pair0(a):
+            for h in (1, 0):
+                for e in range(2):
+                    turn_half(h, 0, e, part[0, a][:, e, h * VH : (h + 1) * VH])
+
+        def first_sum(j, a):
+            nc.gpsimd.tensor_tensor(
+                part[j, a][:],
+                picked[j, a][:, 0].rearrange("p v e -> p e v"),
+                picked[j, a][:, 1].rearrange("p v e -> p e v"),
                 ADD,
             )
+
+        def words(x):
+            return x.rearrange("p v u e -> p (v u e)").bitcast(F32).rearrange("p (v u) -> p v u", u=2)
+
+        def turn_back(dst, src):
+            nc.tensor.transpose(dst, src.rearrange("v p e -> v (p e)").bitcast(F32), ident[:])
 
         def quantize_x(g, v0, v1, src):
             nc.vector.quantize_mx(
@@ -109,50 +133,57 @@ def tile_picked_hash_lin_none_sub_l_kernel(tc, xT, w, offs, out):
 
         fill(nc.scalar.copy, 0, 0, CUT)
         fill(nc.vector.tensor_copy, 0, CUT, T)
-        for j in (1, 2, 3):
-            for c0, c1 in PIECES:
-                fill(nc.scalar.copy, j, c0, c1)
-        for j in range(2):
-            for a in range(2):
-                gather(j, a)
-                nc.gpsimd.tensor_tensor(
-                    part[j, a][:],
-                    picked[j, a][:, 0].rearrange("p v e -> p e v"),
-                    picked[j, a][:, 1].rearrange("p v e -> p e v"),
-                    ADD,
-                )
+        gather(0, 0)
+        first_sum(0, 0)
+        gather_single(0, True, 0, keep.tile([P, 3 * VH], F32, name="got0", align_bytes=64))
+        gather(0, 1)
+        first_sum(0, 1)
+        turn_pair0(0)
+        gather_single(0, False, 3, pair[0][:, 0, 0 : 4 * VH])
+        turn_pair0(1)
+        for c0, c1 in PIECES:
+            fill(nc.scalar.copy, 1, c0, c1)
+        gather_single(0, True, 7, keep.tile([P, VH], F32, name="got0_last", align_bytes=64))
+        gather_single(1, True, 0, keep.tile([P, 3 * VH], F32, name="got1", align_bytes=64))
+        fill(nc.scalar.copy, 2, 0, CUT)
         for a in range(2):
-            gather(2, a)
-            nc.gpsimd.tensor_tensor(part23[:, 0, a], picked[2, a][:, 0], picked[2, a][:, 1], ADD)
-        for a in range(2):
-            gather(3, a)
-        spent = pair[3][:, 0, HALF:T].bitcast(BF16).rearrange("v (u h p e) -> v u h p e", u=2, h=2, e=2)
-        rounded = [spent[:, u] for u in range(2)]
-        w_bf = pair[3][:, 0, 0:HALF].bitcast(BF16).rearrange("p (g m t) -> p g m t", g=PASSES, t=4)
-        for u in range(2):
-            for e in range(2):
-                turn_and_add(u, e, [part[u, a][:, e] for a in range(2)])
-            nc.scalar.copy(rounded[u], turned[u][:].rearrange("v h e p -> v h p e"))
-        back = psum.tile([P, 2, V], F32, name="back")
-        for u in range(2):
-            turn_back(u)
+            gather(1, a)
+            nc.gpsimd.tensor_tensor(part12[:, 0, a], picked[1, a][:, 0], picked[1, a][:, 1], ADD)
+        gather_single(1, False, 3, pair[1][:, 0, T - 2 * VH : T])
+        fill(nc.scalar.copy, 2, CUT, T)
+        gather_single(1, True, 5, pair[2][:, 0, T - 3 * VH : T])
+        gather(2, 0)
+        nc.gpsimd.tensor_tensor(part12[:, 1, 0], picked[2, 0][:, 0], picked[2, 0][:, 1], ADD)
+        gather(2, 1)
+        nc.vector.tensor_tensor(part12[:, 1, 1], picked[2, 1][:, 0], picked[2, 1][:, 1], ADD)
+
+        w_bf = pair[2][:, 0, T - 3 * VH - HALF : T - 3 * VH].bitcast(BF16).rearrange("p (g m t) -> p g m t", g=PASSES, t=4)
         nc.scalar.copy(w_bf, w_raw[:].rearrange("p g t m -> p g m t"))
-        nc.scalar.copy(
-            x_bf0[:].rearrange("p v u e -> p (v u e)").bitcast(F32).rearrange("p (v u) -> p v u", u=2),
-            back[:].rearrange("p u v -> p v u"),
-        )
-        for a in range(2):
-            nc.vector.tensor_tensor(part23[:, 1, a], picked[3, a][:, 0], picked[3, a][:, 1], ADD)
-        w_codes = keep.tile([P, PASSES, M], U32, name="w_codes", tag="picked3_0", align_bytes=64)
+        rounded = [keep.tile([P, 2, P, 2], BF16, name=f"rounded_h{h}", align_bytes=64) for h in range(2)]
+        back0 = psum.tile([P, 2, V], F32, name="back0")
+        for h in (1, 0):
+            nc.scalar.copy(rounded[h][:], turned[h][:].rearrange("v u e p -> v u p e"))
+            for u in range(2):
+                turn_back(back0[:, u, h * VH : (h + 1) * VH], rounded[h][:, u])
+        nc.scalar.copy(words(x_bf0[:]), back0[:].rearrange("p u v -> p v u"))
+
+        w_codes = at([P, PASSES, M], U32, "w_codes", 4)
+        x_codes = {1: keep.tile([P, V], U32, name="x_codes1", align_bytes=64)}
         nc.vector.quantize_mx(
             out=w_codes[:].rearrange("p g m -> p (g m)").bitcast(FP8X4),
             scales=w_scales[:].rearrange("p g m -> p (g m)"),
             in_=w_bf.rearrange("p g m t -> p (g m t)"),
         )
-        finish(1)
-        finish(0)
+        for h in (1, 0):
+            ids = slice(h * VH, (h + 1) * VH)
+            nc.vector.tensor_tensor(
+                x_bf1[h][:],
+                part12[:, :, 0, ids].rearrange("p u v e -> p v u e"),
+                part12[:, :, 1, ids].rearrange("p u v e -> p v u e"),
+                ADD,
+            )
         quantize_x(1, VH, V, x_bf1[1][:])
-        x_codes[0] = keep.tile([P, V], U32, name="x_codes0", tag="part23", align_bytes=64)
+        x_codes[0] = keep.tile([P, V], U32, name="x_codes0", tag="part12", align_bytes=64)
         quantize_x(0, VH, V, x_bf0[:, VH:V])
         quantize_x(1, 0, VH, x_bf1[0][:])
         quantize_x(0, 0, VH, x_bf0[:, 0:VH])

@@ -21,7 +21,6 @@ HALF = T // 2
 VH = V // 2
 CUT = 576
 PIECES = ((0, CUT), (CUT, T))
-PAIR_ROWS = ((0, 0), (1, 0), (1, 1))
 
 
 def tile_picked_hash_lin_none_sub_l_kernel(tc, xT, w, offs, out):
@@ -33,34 +32,36 @@ def tile_picked_hash_lin_none_sub_l_kernel(tc, xT, w, offs, out):
 
         offsets = keep.tile([P, D * V // 16], U16, name="offsets")
         rows = xT.rearrange("(g p u e) c -> g u p e c", g=PASSES, u=2, e=2)
-        pair = [keep.tile([P, 2, T], F32, name=f"pair{j}", align_bytes=64) for j in range(3)]
-        single = [keep.tile([P, T], F32, name=f"single{e}", align_bytes=64) for e in range(2)]
+        pair = [keep.tile([P, 2, T], F32, name=f"pair{j}", align_bytes=64) for j in range(2)]
+        single = {(g, e): keep.tile([P, T], F32, name=f"single{g}_{e}", align_bytes=64) for g in range(2) for e in range(2)}
         w_raw = keep.tile([P, PASSES, 4, M], F32, name="w_raw")
-        for j in range(3):
+        nc.sync.dma_start(out=single[0, 0][:], in_=rows[0, 0, :, 0, :])
+        nc.sync.dma_start(offsets[:], offs)
+        nc.sync.dma_start(out=single[0, 1][:], in_=rows[0, 0, :, 1, :])
+        for j in range(2):
             for c0, c1 in PIECES:
                 cols = slice(c0, c1)
-                nc.sync.dma_start(out=pair[j][:, :, cols], in_=rows[PAIR_ROWS[j][0], PAIR_ROWS[j][1], :, :, cols])
-            if j == 0:
-                nc.sync.dma_start(offsets[:], offs)
-            if j < 2:
-                nc.sync.dma_start(out=single[j][:], in_=rows[0, 1, :, j, :])
+                nc.sync.dma_start(out=pair[j][:, :, cols], in_=rows[1, j, :, :, cols])
+            nc.sync.dma_start(out=single[1, j][:], in_=rows[0, 1, :, j, :])
         nc.sync.dma_start(out=w_raw[:], in_=w.rearrange("(g p t) m -> p g t m", g=PASSES, t=4))
 
         ident = keep.tile([P, P], F32, name="ident")
-        make_identity(nc, ident[:])
+        zeros = keep.tile([P, P], F32, name="zeros")
+        nc.vector.memset(zeros[:], 0.0)
+        nc.scalar.copy(ident[:], zeros[:])
+        make_identity(nc, ident[:], nomemset=True)
 
         def at(shape, dtype, name, slot, skip=0):
             return ring.tile(shape, dtype, name=name, offset=2048 * slot + skip, align_bytes=64)
 
-        picked = {(j, a): at([P, 2, V, 2], BF16, f"picked{j}_{a}", 2 * j + a) for j in range(3) for a in range(2)}
-        part = {(j, a): at([P, 2, V], F32, f"part{j}_{a}", 6 + 2 * j + a) for j in range(1) for a in range(2)}
-        part12 = keep.tile([P, 2, 2, V, 2], F32, name="part12", align_bytes=64)
+        picked = {(j, a): at([P, 2, V, 2], BF16, f"picked{j}_{a}", 2 * j + a) for j in range(2) for a in range(2)}
+        sums = [keep.tile([P, 2, V, 2], F32, name=f"sums{a}", align_bytes=64) for a in range(2)]
         turned = [psum.tile([P, 2, 2, P], F32, name=f"turned_h{h}") for h in range(2)]
-        x_bf0 = keep.tile([P, V, 2, 2], BF16, name="x_bf0", align_bytes=64)
-        x_bf1 = [keep.tile([P, VH, 2, 2], BF16, name=f"x_bf1_{h}", align_bytes=64) for h in range(2)]
+        x_bf0 = [keep.tile([P, VH, 2, 2], BF16, name=f"x_bf0_{h}", align_bytes=64) for h in range(2)]
+        last_row = single[1, 1][:].bitcast(BF16).rearrange("p (h v u e) -> p h v u e", v=VH, u=2, e=2)
+        x_bf1 = [last_row[:, 3 * h] for h in range(2)]
         x_scales = keep.tile([P, PASSES, V], U8, name="x_scales", align_bytes=64)
         w_scales = keep.tile([P, PASSES, M], U8, name="w_scales", align_bytes=64)
-        acc = [psum.tile([M, VH], F32, name=f"acc{h}") for h in range(2)]
         result = [keep.tile([M, VH], F32, name=f"result{h}") for h in range(2)]
 
         def entries(first, count):
@@ -79,32 +80,18 @@ def tile_picked_hash_lin_none_sub_l_kernel(tc, xT, w, offs, out):
         def turn_half(h, u, e, term):
             nc.tensor.matmul(
                 turned[h][:, u, e, :], term, ident[:],
-                is_transpose=True, start=(done.count(h) == 0), stop=(done.count(h) == 2 * D + 3),
+                is_transpose=True, start=(done.count(h) == 0), stop=(done.count(h) == 4 * D - 1),
             )
             done.append(h)
 
-        def gather_single(e, on_scalar, r0, got):
-            n = got.shape[1] // VH
-            window = single[e][:].indirect(entries(r0 * VH, n * VH))
+        def look_up(on_scalar, u, e, r0, got):
+            window = single[u, e][:].indirect(entries(r0 * VH, got.shape[1]))
             if on_scalar:
-                nc.scalar.activation(got[:, :], window, COPY)
+                nc.scalar.activation(got, window, COPY)
             else:
-                nc.vector.tensor_copy(got[:, :], window)
-            for r in range(n):
-                turn_half((r0 + r) % 2, 1, e, got[:, r * VH : (r + 1) * VH])
-
-        def turn_pair0(a):
-            for h in (1, 0):
-                for e in range(2):
-                    turn_half(h, 0, e, part[0, a][:, e, h * VH : (h + 1) * VH])
-
-        def first_sum(j, a):
-            nc.gpsimd.tensor_tensor(
-                part[j, a][:],
-                picked[j, a][:, 0].rearrange("p v e -> p e v"),
-                picked[j, a][:, 1].rearrange("p v e -> p e v"),
-                ADD,
-            )
+                nc.vector.tensor_copy(got, window)
+            for r in reversed(range(got.shape[1] // VH)):
+                turn_half((r0 + r) % 2, u, e, got[:, r * VH : (r + 1) * VH])
 
         def words(x):
             return x.rearrange("p v u e -> p (v u e)").bitcast(F32).rearrange("p (v u) -> p v u", u=2)
@@ -131,62 +118,68 @@ def tile_picked_hash_lin_none_sub_l_kernel(tc, xT, w, offs, out):
                 stop=not first,
             )
 
+        picks = {(u, e): keep.tile([P, T], F32, name=f"picks{u}_{e}", align_bytes=64) for u in range(2) for e in range(2)}
+
+        def runs(tile, r0, r1):
+            return tile[:, r0 * VH : r1 * VH]
+
+        look_up(True, 0, 0, 0, runs(picks[0, 0], 0, 2))
+        look_up(False, 0, 0, 2, runs(picks[0, 0], 2, 8))
+        look_up(True, 0, 1, 0, runs(picks[0, 1], 0, 4))
+        look_up(False, 0, 1, 4, runs(picks[0, 1], 4, 8))
         fill(nc.scalar.copy, 0, 0, CUT)
         fill(nc.vector.tensor_copy, 0, CUT, T)
-        gather(0, 0)
-        first_sum(0, 0)
-        gather_single(0, True, 0, keep.tile([P, 3 * VH], F32, name="got0", align_bytes=64))
-        gather(0, 1)
-        first_sum(0, 1)
-        turn_pair0(0)
-        gather_single(0, False, 3, pair[0][:, 0, 0 : 4 * VH])
-        turn_pair0(1)
+        for a in range(2):
+            gather(0, a)
+            nc.gpsimd.tensor_tensor(sums[a][:, 0], picked[0, a][:, 0], picked[0, a][:, 1], ADD)
+        look_up(True, 1, 0, 0, runs(picks[1, 0], 0, 4))
+        look_up(False, 1, 0, 5, runs(pair[0][:, 0], 0, 3))
         for c0, c1 in PIECES:
             fill(nc.scalar.copy, 1, c0, c1)
-        gather_single(0, True, 7, keep.tile([P, VH], F32, name="got0_last", align_bytes=64))
-        gather_single(1, True, 0, keep.tile([P, 3 * VH], F32, name="got1", align_bytes=64))
-        fill(nc.scalar.copy, 2, 0, CUT)
-        for a in range(2):
-            gather(1, a)
-            nc.gpsimd.tensor_tensor(part12[:, 0, a], picked[1, a][:, 0], picked[1, a][:, 1], ADD)
-        gather_single(1, False, 3, pair[1][:, 0, T - 2 * VH : T])
-        fill(nc.scalar.copy, 2, CUT, T)
-        gather_single(1, True, 5, pair[2][:, 0, T - 3 * VH : T])
-        gather(2, 0)
-        nc.gpsimd.tensor_tensor(part12[:, 1, 0], picked[2, 0][:, 0], picked[2, 0][:, 1], ADD)
-        gather(2, 1)
-        nc.vector.tensor_tensor(part12[:, 1, 1], picked[2, 1][:, 0], picked[2, 1][:, 1], ADD)
+        gather(1, 0)
+        nc.gpsimd.tensor_tensor(sums[0][:, 1], picked[1, 0][:, 0], picked[1, 0][:, 1], ADD)
+        gather(1, 1)
+        for d in range(D - 1):
+            look_up(True, 1, 1, 2 * d, runs(picks[1, 1], 2 * d, 2 * d + 2))
+        look_up(False, 1, 0, 4, runs(pair[1][:, 0], 7, 8))
+        look_up(True, 1, 1, 6, runs(picks[1, 1], 6, 8))
+        for h in (1, 0):
+            ids = slice(h * VH, (h + 1) * VH)
+            nc.vector.tensor_tensor(sums[1][:, 1, ids], picked[1, 1][:, 0, ids], picked[1, 1][:, 1, ids], ADD)
 
-        w_bf = pair[2][:, 0, T - 3 * VH - HALF : T - 3 * VH].bitcast(BF16).rearrange("p (g m t) -> p g m t", g=PASSES, t=4)
-        nc.scalar.copy(w_bf, w_raw[:].rearrange("p g t m -> p g m t"))
-        rounded = [keep.tile([P, 2, P, 2], BF16, name=f"rounded_h{h}", align_bytes=64) for h in range(2)]
-        back0 = psum.tile([P, 2, V], F32, name="back0")
+        w_bf = single[1, 1][:, HALF - 2 * M : HALF + 2 * M].bitcast(BF16).rearrange("p (g m t) -> p g m t", g=PASSES, t=4)
+        rounded = [keep.tile([P, 2, P, 2], BF16, name=f"rounded{h}", align_bytes=64) for h in range(2)]
+        back = [psum.tile([P, 2, VH], F32, name=f"back{h}") for h in range(2)]
+        nc.scalar.copy(w_bf[:, 0], w_raw[:, 0].rearrange("p t m -> p m t"))
         for h in (1, 0):
             nc.scalar.copy(rounded[h][:], turned[h][:].rearrange("v u e p -> v u p e"))
             for u in range(2):
-                turn_back(back0[:, u, h * VH : (h + 1) * VH], rounded[h][:, u])
-        nc.scalar.copy(words(x_bf0[:]), back0[:].rearrange("p u v -> p v u"))
+                turn_back(back[h][:, u], rounded[h][:, u])
+        for h in (1, 0):
+            nc.scalar.copy(words(x_bf0[h][:]), back[h][:].rearrange("p u v -> p v u"))
 
-        w_codes = at([P, PASSES, M], U32, "w_codes", 4)
+        for h in (1, 0):
+            ids = slice(h * VH, (h + 1) * VH)
+            nc.vector.tensor_tensor(
+                x_bf1[h],
+                sums[0][:, :, ids].rearrange("p u v e -> p v u e"),
+                sums[1][:, :, ids].rearrange("p u v e -> p v u e"),
+                ADD,
+            )
+        nc.vector.tensor_copy(w_bf[:, 1], w_raw[:, 1].rearrange("p t m -> p m t"))
         x_codes = {1: keep.tile([P, V], U32, name="x_codes1", align_bytes=64)}
+        quantize_x(1, VH, V, x_bf1[1])
+        quantize_x(1, 0, VH, x_bf1[0])
+        w_codes = keep.tile([P, PASSES, M], U32, name="w_codes", tag="sums0", align_bytes=64)
         nc.vector.quantize_mx(
             out=w_codes[:].rearrange("p g m -> p (g m)").bitcast(FP8X4),
             scales=w_scales[:].rearrange("p g m -> p (g m)"),
             in_=w_bf.rearrange("p g m t -> p (g m t)"),
         )
-        for h in (1, 0):
-            ids = slice(h * VH, (h + 1) * VH)
-            nc.vector.tensor_tensor(
-                x_bf1[h][:],
-                part12[:, :, 0, ids].rearrange("p u v e -> p v u e"),
-                part12[:, :, 1, ids].rearrange("p u v e -> p v u e"),
-                ADD,
-            )
-        quantize_x(1, VH, V, x_bf1[1][:])
-        x_codes[0] = keep.tile([P, V], U32, name="x_codes0", tag="part12", align_bytes=64)
-        quantize_x(0, VH, V, x_bf0[:, VH:V])
-        quantize_x(1, 0, VH, x_bf1[0][:])
-        quantize_x(0, 0, VH, x_bf0[:, 0:VH])
+        x_codes[0] = keep.tile([P, V], U32, name="x_codes0", tag="sums1", align_bytes=64)
+        quantize_x(0, VH, V, x_bf0[1][:])
+        quantize_x(0, 0, VH, x_bf0[0][:])
+        acc = [psum.tile([M, VH], F32, name=f"acc{h}", tag=f"back{h}") for h in range(2)]
         for h in (1, 0):
             multiply(1, h, True)
             multiply(0, h, False)

@@ -41,7 +41,7 @@ def tile_picked_hash_lin_none_sub_l_kernel(tc, xT, w, offs, out):
         for j in range(2):
             for c0, c1 in PIECES:
                 cols = slice(c0, c1)
-                nc.sync.dma_start(out=pair[j][:, :, cols], in_=rows[1, j, :, :, cols])
+                nc.sync.dma_start(out=pair[j][:, :, cols], in_=rows[1, 1 - j, :, :, cols])
             nc.sync.dma_start(out=single[1, j][:], in_=rows[0, 1, :, j, :])
         nc.sync.dma_start(out=w_raw[:], in_=w.rearrange("(g p t) m -> p g t m", g=PASSES, t=4))
 
@@ -55,11 +55,12 @@ def tile_picked_hash_lin_none_sub_l_kernel(tc, xT, w, offs, out):
             return ring.tile(shape, dtype, name=name, offset=2048 * slot + skip, align_bytes=64)
 
         picked = {(j, a): at([P, 2, V, 2], BF16, f"picked{j}_{a}", 2 * j + a) for j in range(2) for a in range(2)}
-        sums = [keep.tile([P, 2, V, 2], F32, name=f"sums{a}", align_bytes=64) for a in range(2)]
+        sums0 = keep.tile([P, 2, V, 2], F32, name="sums0", align_bytes=64)
+        sums = [sums0[:], pair[1][:, 0].rearrange("p (u v e) -> p u v e", u=2, e=2)]
         turned = [psum.tile([P, 2, 2, P], F32, name=f"turned_h{h}") for h in range(2)]
         x_bf0 = [keep.tile([P, VH, 2, 2], BF16, name=f"x_bf0_{h}", align_bytes=64) for h in range(2)]
         last_row = single[1, 1][:].bitcast(BF16).rearrange("p (h v u e) -> p h v u e", v=VH, u=2, e=2)
-        x_bf1 = [last_row[:, 3 * h] for h in range(2)]
+        x_bf1 = [last_row[:, h] for h in range(2)]
         x_scales = keep.tile([P, PASSES, V], U8, name="x_scales", align_bytes=64)
         w_scales = keep.tile([P, PASSES, M], U8, name="w_scales", align_bytes=64)
         result = [keep.tile([M, VH], F32, name=f"result{h}") for h in range(2)]
@@ -131,26 +132,31 @@ def tile_picked_hash_lin_none_sub_l_kernel(tc, xT, w, offs, out):
         fill(nc.vector.tensor_copy, 0, CUT, T)
         for a in range(2):
             gather(0, a)
-            nc.gpsimd.tensor_tensor(sums[a][:, 0], picked[0, a][:, 0], picked[0, a][:, 1], ADD)
+        nc.gpsimd.tensor_tensor(sums[0][:, 1], picked[0, 0][:, 0], picked[0, 0][:, 1], ADD)
         look_up(True, 1, 0, 0, runs(picks[1, 0], 0, 4))
-        look_up(False, 1, 0, 5, runs(pair[0][:, 0], 0, 3))
-        for c0, c1 in PIECES:
-            fill(nc.scalar.copy, 1, c0, c1)
+        look_up(False, 1, 0, 7, runs(pair[0][:, 0], 0, 1))
+        fill(nc.scalar.copy, 1, 0, CUT)
+        look_up(True, 1, 0, 4, runs(pair[1][:, 0], 0, 3))
+        fill(nc.vector.tensor_copy, 1, CUT, T)
+        nc.gpsimd.tensor_tensor(sums[1][:, 1], picked[0, 1][:, 0], picked[0, 1][:, 1], ADD)
         gather(1, 0)
-        nc.gpsimd.tensor_tensor(sums[0][:, 1], picked[1, 0][:, 0], picked[1, 0][:, 1], ADD)
+        nc.gpsimd.tensor_tensor(sums[0][:, 0], picked[1, 0][:, 0], picked[1, 0][:, 1], ADD)
         gather(1, 1)
         for d in range(D - 1):
             look_up(True, 1, 1, 2 * d, runs(picks[1, 1], 2 * d, 2 * d + 2))
-        look_up(False, 1, 0, 4, runs(pair[1][:, 0], 7, 8))
         look_up(True, 1, 1, 6, runs(picks[1, 1], 6, 8))
         for h in (1, 0):
             ids = slice(h * VH, (h + 1) * VH)
-            nc.vector.tensor_tensor(sums[1][:, 1, ids], picked[1, 1][:, 0, ids], picked[1, 1][:, 1, ids], ADD)
+            nc.vector.tensor_tensor(sums[1][:, 0, ids], picked[1, 1][:, 0, ids], picked[1, 1][:, 1, ids], ADD)
 
-        w_bf = single[1, 1][:, HALF - 2 * M : HALF + 2 * M].bitcast(BF16).rearrange("p (g m t) -> p g m t", g=PASSES, t=4)
+        w_bf = single[1, 1][:, HALF:T].bitcast(BF16).rearrange("p (g m t) -> p g m t", g=PASSES, t=4)
+
+        def cast_weights(copy, g):
+            copy(w_bf[:, g].rearrange("p (c i) t -> p c t i", i=4), w_raw[:, g].rearrange("p t (c i) -> p c t i", i=4))
+
         rounded = [keep.tile([P, 2, P, 2], BF16, name=f"rounded{h}", align_bytes=64) for h in range(2)]
         back = [psum.tile([P, 2, VH], F32, name=f"back{h}") for h in range(2)]
-        nc.scalar.copy(w_bf[:, 0], w_raw[:, 0].rearrange("p t m -> p m t"))
+        cast_weights(nc.scalar.copy, 0)
         for h in (1, 0):
             nc.scalar.copy(rounded[h][:], turned[h][:].rearrange("v u e p -> v u p e"))
             for u in range(2):
@@ -166,22 +172,22 @@ def tile_picked_hash_lin_none_sub_l_kernel(tc, xT, w, offs, out):
                 sums[1][:, :, ids].rearrange("p u v e -> p v u e"),
                 ADD,
             )
-        nc.vector.tensor_copy(w_bf[:, 1], w_raw[:, 1].rearrange("p t m -> p m t"))
+        cast_weights(nc.vector.tensor_copy, 1)
         x_codes = {1: keep.tile([P, V], U32, name="x_codes1", align_bytes=64)}
-        quantize_x(1, VH, V, x_bf1[1])
-        quantize_x(1, 0, VH, x_bf1[0])
+        quantize_x(1, 0, V, last_row[:, 0:2].rearrange("p h v u e -> p (h v) u e"))
         w_codes = keep.tile([P, PASSES, M], U32, name="w_codes", tag="sums0", align_bytes=64)
         nc.vector.quantize_mx(
             out=w_codes[:].rearrange("p g m -> p (g m)").bitcast(FP8X4),
             scales=w_scales[:].rearrange("p g m -> p (g m)"),
             in_=w_bf.rearrange("p g m t -> p (g m t)"),
         )
-        x_codes[0] = keep.tile([P, V], U32, name="x_codes0", tag="sums1", align_bytes=64)
+        x_codes[0] = keep.tile([P, V], U32, name="x_codes0", tag="pair1", align_bytes=64)
         quantize_x(0, VH, V, x_bf0[1][:])
         quantize_x(0, 0, VH, x_bf0[0][:])
-        acc = [psum.tile([M, VH], F32, name=f"acc{h}", tag=f"back{h}") for h in range(2)]
+        acc = [psum.tile([M, VH], F32, name=f"acc{h}", tag=("turned_h0", "back1")[h]) for h in range(2)]
         for h in (1, 0):
             multiply(1, h, True)
+        for h in (1, 0):
             multiply(0, h, False)
         nc.scalar.copy(result[1][:], acc[1][:])
         nc.vector.tensor_copy(result[0][:], acc[0][:])

@@ -59,8 +59,7 @@ def tile_picked_hash_lin_none_sub_l_kernel(tc, xT, w, offs, out):
         sums = [sums0[:], pair[1][:, 0].rearrange("p (u v e) -> p u v e", u=2, e=2)]
         turned = [psum.tile([P, 2, 2, P], F32, name=f"turned_h{h}") for h in range(2)]
         x_bf0 = [keep.tile([P, VH, 2, 2], BF16, name=f"x_bf0_{h}", align_bytes=64) for h in range(2)]
-        last_row = single[1, 1][:].bitcast(BF16).rearrange("p (h v u e) -> p h v u e", v=VH, u=2, e=2)
-        x_bf1 = [last_row[:, h] for h in range(2)]
+        x_bf1 = keep.tile([P, V, 2, 2], BF16, name="x_bf1", align_bytes=64)
         x_scales = keep.tile([P, PASSES, V], U8, name="x_scales", align_bytes=64)
         w_scales = keep.tile([P, PASSES, M], U8, name="w_scales", align_bytes=64)
         result = [keep.tile([M, VH], F32, name=f"result{h}") for h in range(2)]
@@ -142,21 +141,16 @@ def tile_picked_hash_lin_none_sub_l_kernel(tc, xT, w, offs, out):
         gather(1, 0)
         nc.gpsimd.tensor_tensor(sums[0][:, 0], picked[1, 0][:, 0], picked[1, 0][:, 1], ADD)
         gather(1, 1)
-        for d in range(D - 1):
-            look_up(True, 1, 1, 2 * d, runs(picks[1, 1], 2 * d, 2 * d + 2))
-        look_up(True, 1, 1, 6, runs(picks[1, 1], 6, 8))
+        for r0, r1 in ((0, 2), (2, 4), (4, 6), (7, 8), (6, 7)):
+            look_up(True, 1, 1, r0, runs(picks[1, 1], r0, r1))
         for h in (1, 0):
             ids = slice(h * VH, (h + 1) * VH)
             nc.vector.tensor_tensor(sums[1][:, 0, ids], picked[1, 1][:, 0, ids], picked[1, 1][:, 1, ids], ADD)
 
         w_bf = single[1, 1][:, HALF:T].bitcast(BF16).rearrange("p (g m t) -> p g m t", g=PASSES, t=4)
 
-        def cast_weights(copy, g):
-            copy(w_bf[:, g].rearrange("p (c i) t -> p c t i", i=4), w_raw[:, g].rearrange("p t (c i) -> p c t i", i=4))
-
         rounded = [keep.tile([P, 2, P, 2], BF16, name=f"rounded{h}", align_bytes=64) for h in range(2)]
         back = [psum.tile([P, 2, VH], F32, name=f"back{h}") for h in range(2)]
-        cast_weights(nc.scalar.copy, 0)
         for h in (1, 0):
             nc.scalar.copy(rounded[h][:], turned[h][:].rearrange("v u e p -> v u p e"))
             for u in range(2):
@@ -167,14 +161,16 @@ def tile_picked_hash_lin_none_sub_l_kernel(tc, xT, w, offs, out):
         for h in (1, 0):
             ids = slice(h * VH, (h + 1) * VH)
             nc.vector.tensor_tensor(
-                x_bf1[h],
+                x_bf1[:, ids],
                 sums[0][:, :, ids].rearrange("p u v e -> p v u e"),
                 sums[1][:, :, ids].rearrange("p u v e -> p v u e"),
                 ADD,
             )
-        cast_weights(nc.vector.tensor_copy, 1)
+        nc.vector.tensor_copy(
+            w_bf.rearrange("p g (c i) t -> p g c t i", i=4), w_raw[:].rearrange("p g t (c i) -> p g c t i", i=4)
+        )
         x_codes = {1: keep.tile([P, V], U32, name="x_codes1", align_bytes=64)}
-        quantize_x(1, 0, V, last_row[:, 0:2].rearrange("p h v u e -> p (h v) u e"))
+        quantize_x(1, 0, V, x_bf1[:])
         w_codes = keep.tile([P, PASSES, M], U32, name="w_codes", tag="sums0", align_bytes=64)
         nc.vector.quantize_mx(
             out=w_codes[:].rearrange("p g m -> p (g m)").bitcast(FP8X4),

@@ -149,6 +149,14 @@ def tile_picked_hash_lin_none_sub_l_kernel(tc, xT, w, offs, out):
 
         w_bf = single[1, 1][:, HALF:T].bitcast(BF16).rearrange("p (g m t) -> p g m t", g=PASSES, t=4)
 
+
+        def cast_weights(copy, cols):
+            copy(
+                w_bf[:, :, cols].rearrange("p g (c i) t -> p g c t i", i=4),
+                w_raw[:, :, :, cols].rearrange("p g t (c i) -> p g c t i", i=4),
+            )
+
+        cast_weights(nc.scalar.copy, slice(0, M // 4))
         rounded = [keep.tile([P, 2, P, 2], BF16, name=f"rounded{h}", align_bytes=64) for h in range(2)]
         back = [psum.tile([P, 2, VH], F32, name=f"back{h}") for h in range(2)]
         for h in (1, 0):
@@ -166,9 +174,7 @@ def tile_picked_hash_lin_none_sub_l_kernel(tc, xT, w, offs, out):
                 sums[1][:, :, ids].rearrange("p u v e -> p v u e"),
                 ADD,
             )
-        nc.vector.tensor_copy(
-            w_bf.rearrange("p g (c i) t -> p g c t i", i=4), w_raw[:].rearrange("p g t (c i) -> p g c t i", i=4)
-        )
+        cast_weights(nc.vector.tensor_copy, slice(M // 4, M))
         x_codes = {1: keep.tile([P, V], U32, name="x_codes1", align_bytes=64)}
         quantize_x(1, 0, V, x_bf1[:])
         w_codes = keep.tile([P, PASSES, M], U32, name="w_codes", tag="sums0", align_bytes=64)

@@ -17,32 +17,25 @@ COPY = mybir.ActivationFunctionType.Copy
 
 P = 128
 PASSES = 2
-HALF = T // 2
 VH = V // 2
-CUT = 576
-PIECES = ((0, CUT), (CUT, T))
+CUT = 480
 
 
 def tile_picked_hash_lin_none_sub_l_kernel(tc, xT, w, offs, out):
     nc = tc.nc
     with ExitStack() as ctx:
         keep = ctx.enter_context(tc.tile_pool(name="keep", bufs=1))
-        ring = ctx.enter_context(tc.tile_pool(name="ring", bufs=1))
         psum = ctx.enter_context(tc.psum_pool(name="psum", bufs=1))
 
         offsets = keep.tile([P, D * V // 16], U16, name="offsets")
-        rows = xT.rearrange("(g p u e) c -> g u p e c", g=PASSES, u=2, e=2)
-        pair = [keep.tile([P, 2, T], F32, name=f"pair{j}", align_bytes=64) for j in range(2)]
-        single = {(g, e): keep.tile([P, T], F32, name=f"single{g}_{e}", align_bytes=64) for g in range(2) for e in range(2)}
+        rows = xT.rearrange("(g p t) c -> g t p c", g=PASSES, t=4)
+        table = {(g, t): keep.tile([P, T], F32, name=f"table{g}_{t}", align_bytes=64) for g in range(PASSES) for t in range(4)}
         w_raw = keep.tile([P, PASSES, 4, M], F32, name="w_raw")
-        nc.sync.dma_start(out=single[0, 0][:], in_=rows[0, 0, :, 0, :])
-        nc.sync.dma_start(offsets[:], offs)
-        nc.sync.dma_start(out=single[0, 1][:], in_=rows[0, 0, :, 1, :])
-        for j in range(2):
-            for c0, c1 in PIECES:
-                cols = slice(c0, c1)
-                nc.sync.dma_start(out=pair[j][:, :, cols], in_=rows[1, 1 - j, :, :, cols])
-            nc.sync.dma_start(out=single[1, j][:], in_=rows[0, 1, :, j, :])
+        for g in range(PASSES):
+            for t in range(4):
+                nc.sync.dma_start(out=table[g, t][:], in_=rows[g, t])
+                if (g, t) == (0, 0):
+                    nc.sync.dma_start(offsets[:], offs)
         nc.sync.dma_start(out=w_raw[:], in_=w.rearrange("(g p t) m -> p g t m", g=PASSES, t=4))
 
         ident = keep.tile([P, P], F32, name="ident")
@@ -51,146 +44,109 @@ def tile_picked_hash_lin_none_sub_l_kernel(tc, xT, w, offs, out):
         nc.scalar.copy(ident[:], zeros[:])
         make_identity(nc, ident[:], nomemset=True)
 
-        def at(shape, dtype, name, slot, skip=0):
-            return ring.tile(shape, dtype, name=name, offset=2048 * slot + skip, align_bytes=64)
+        def look_up(on_scalar, g, t, r0, r1):
+            got = keep.tile([P, (r1 - r0) * VH], F32, name=f"got{g}_{t}_{r0}", align_bytes=64)
+            window = table[g, t][:].indirect(offsets[:, r0 * VH // 16 : r1 * VH // 16])
+            if on_scalar:
+                nc.scalar.activation(got[:], window, COPY)
+            else:
+                nc.vector.tensor_copy(got[:], window)
+            return got
 
-        picked = {(j, a): at([P, 2, V, 2], BF16, f"picked{j}_{a}", 2 * j + a) for j in range(2) for a in range(2)}
-        sums0 = keep.tile([P, 2, V, 2], F32, name="sums0", align_bytes=64)
-        sums = [sums0[:], pair[1][:, 0].rearrange("p (u v e) -> p u v e", u=2, e=2)]
-        turned = [psum.tile([P, 2, 2, P], F32, name=f"turned_h{h}") for h in range(2)]
-        x_bf0 = [keep.tile([P, VH, 2, 2], BF16, name=f"x_bf0_{h}", align_bytes=64) for h in range(2)]
-        x_bf1 = keep.tile([P, V, 2, 2], BF16, name="x_bf1", align_bytes=64)
-        x_scales = keep.tile([P, PASSES, V], U8, name="x_scales", align_bytes=64)
-        w_scales = keep.tile([P, PASSES, M], U8, name="w_scales", align_bytes=64)
-        result = [keep.tile([M, VH], F32, name=f"result{h}") for h in range(2)]
+        part = keep.tile([P, 4, 2, V], F32, name="part", align_bytes=64)
+        for t in range(4):
+            got = keep.tile([P, D * V], F32, name=f"got0_{t}", align_bytes=64)
+            nc.scalar.activation(got[:, :CUT], table[0, t][:].indirect(offsets[:, : CUT // 16]), COPY)
+            nc.vector.tensor_copy(got[:, CUT:], table[0, t][:].indirect(offsets[:, CUT // 16 :]))
+            nc.gpsimd.tensor_tensor(part[:, t].rearrange("p a v -> p (a v)"), got[:, : 2 * V], got[:, 2 * V :], ADD)
+        x_bf0 = keep.tile([P, V, 4], BF16, name="x_bf0", align_bytes=64)
+        nc.gpsimd.tensor_tensor(
+            x_bf0[:].rearrange("p (c i) t -> p c t i", i=4),
+            part[:, :, 0].rearrange("p t (c i) -> p c t i", i=4),
+            part[:, :, 1].rearrange("p t (c i) -> p c t i", i=4),
+            ADD,
+        )
 
-        def entries(first, count):
-            return offsets[:, first // 16 : (first + count) // 16]
-
-        def fill(copy, j, c0, c1):
-            halves = pair[j][:, 1].bitcast(BF16).rearrange("p (c e) -> p c e", e=2)
-            copy(halves[:, c0:c1, 0], pair[j][:, 0, c0:c1])
-
-        def gather(j, a):
-            words = picked[j, a][:].rearrange("p d v e -> p (d v e)").bitcast(U32)
-            nc.vector.tensor_copy(words, pair[j][:, 1].bitcast(U32).indirect(entries(2 * a * V, 2 * V)))
-
+        turned = [psum.tile([P, 4, P], F32, name=f"turned_h{h}") for h in range(2)]
         done = []
 
-        def turn_half(h, u, e, term):
+        def turn(t, r, term):
+            h = r % 2
             nc.tensor.matmul(
-                turned[h][:, u, e, :], term, ident[:],
+                turned[h][:, t, :], term, ident[:],
                 is_transpose=True, start=(done.count(h) == 0), stop=(done.count(h) == 4 * D - 1),
             )
             done.append(h)
 
-        def look_up(on_scalar, u, e, r0, got):
-            window = single[u, e][:].indirect(entries(r0 * VH, got.shape[1]))
-            if on_scalar:
-                nc.scalar.activation(got, window, COPY)
-            else:
-                nc.vector.tensor_copy(got, window)
-            for r in reversed(range(got.shape[1] // VH)):
-                turn_half((r0 + r) % 2, u, e, got[:, r * VH : (r + 1) * VH])
+        for t in range(3):
+            for on_scalar, r0 in ((True, 0), (False, 4)):
+                got = look_up(on_scalar, 1, t, r0, r0 + 4)
+                for r in range(4):
+                    turn(t, r0 + r, got[:, r * VH : (r + 1) * VH])
+        last = {}
+        for h in (1, 0):
+            for a in range(2):
+                for on_scalar, d in ((True, a), (False, 2 + a)):
+                    r = 2 * d + h
+                    last[r] = look_up(on_scalar, 1, 3, r, r + 1)
+                    turn(3, r, last[r][:])
 
-        def words(x):
-            return x.rearrange("p v u e -> p (v u e)").bitcast(F32).rearrange("p (v u) -> p v u", u=2)
-
-        def turn_back(dst, src):
-            nc.tensor.transpose(dst, src.rearrange("v p e -> v (p e)").bitcast(F32), ident[:])
+        x_scales = keep.tile([P, PASSES, V], U8, name="x_scales", align_bytes=64)
+        w_scales = keep.tile([P, PASSES, M], U8, name="w_scales", align_bytes=64)
+        w_bf = keep.tile([P, PASSES, M, 4], BF16, name="w_bf", align_bytes=64)
+        w_codes = keep.tile([P, PASSES, M], U32, name="w_codes", align_bytes=64)
+        x_codes = [
+            keep.tile([P, V], U32, name="x_codes0", tag="got1_3_1", align_bytes=64),
+            keep.tile([P, V], U32, name="x_codes1", align_bytes=64),
+        ]
 
         def quantize_x(g, v0, v1, src):
             nc.vector.quantize_mx(
                 out=x_codes[g][:, v0:v1].bitcast(FP8X4),
                 scales=x_scales[:, g, v0:v1],
-                in_=src.rearrange("p v u e -> p (v u e)"),
+                in_=src.rearrange("p v t -> p (v t)"),
             )
 
-        def multiply(g, h, first):
-            ids = slice(h * VH, (h + 1) * VH)
-            nc.tensor.matmul_mx(
-                out=acc[h][:],
-                lhsT=w_codes[:, g, :].bitcast(FP8X4),
-                lhsT_scale=w_scales[:, g, :],
-                rhs=x_codes[g][:, ids].bitcast(FP8X4),
-                rhs_scale=x_scales[:, g, ids],
-                start=first,
-                stop=not first,
-            )
-
-        picks = {(u, e): keep.tile([P, T], F32, name=f"picks{u}_{e}", align_bytes=64) for u in range(2) for e in range(2)}
-
-        def runs(tile, r0, r1):
-            return tile[:, r0 * VH : r1 * VH]
-
-        look_up(True, 0, 0, 0, runs(picks[0, 0], 0, 2))
-        look_up(False, 0, 0, 2, runs(picks[0, 0], 2, 8))
-        look_up(True, 0, 1, 0, runs(picks[0, 1], 0, 4))
-        look_up(False, 0, 1, 4, runs(picks[0, 1], 4, 8))
-        fill(nc.scalar.copy, 0, 0, CUT)
-        fill(nc.vector.tensor_copy, 0, CUT, T)
-        for a in range(2):
-            gather(0, a)
-        nc.gpsimd.tensor_tensor(sums[0][:, 1], picked[0, 0][:, 0], picked[0, 0][:, 1], ADD)
-        look_up(True, 1, 0, 0, runs(picks[1, 0], 0, 4))
-        look_up(False, 1, 0, 7, runs(pair[0][:, 0], 0, 1))
-        fill(nc.scalar.copy, 1, 0, CUT)
-        look_up(True, 1, 0, 4, runs(pair[1][:, 0], 0, 3))
-        fill(nc.vector.tensor_copy, 1, CUT, T)
-        nc.gpsimd.tensor_tensor(sums[1][:, 1], picked[0, 1][:, 0], picked[0, 1][:, 1], ADD)
-        gather(1, 0)
-        nc.gpsimd.tensor_tensor(sums[0][:, 0], picked[1, 0][:, 0], picked[1, 0][:, 1], ADD)
-        gather(1, 1)
-        for r0, r1 in ((0, 2), (2, 4), (4, 6), (7, 8), (6, 7)):
-            look_up(True, 1, 1, r0, runs(picks[1, 1], r0, r1))
-        for h in (1, 0):
-            ids = slice(h * VH, (h + 1) * VH)
-            nc.vector.tensor_tensor(sums[1][:, 0, ids], picked[1, 1][:, 0, ids], picked[1, 1][:, 1, ids], ADD)
-
-        w_bf = single[1, 1][:, HALF:T].bitcast(BF16).rearrange("p (g m t) -> p g m t", g=PASSES, t=4)
-
-
-        def cast_weights(copy, cols):
-            copy(
-                w_bf[:, :, cols].rearrange("p g (c i) t -> p g c t i", i=4),
-                w_raw[:, :, :, cols].rearrange("p g t (c i) -> p g c t i", i=4),
-            )
-
-        cast_weights(nc.scalar.copy, slice(0, M // 4))
-        rounded = [keep.tile([P, 2, P, 2], BF16, name=f"rounded{h}", align_bytes=64) for h in range(2)]
-        back = [psum.tile([P, 2, VH], F32, name=f"back{h}") for h in range(2)]
-        for h in (1, 0):
-            nc.scalar.copy(rounded[h][:], turned[h][:].rearrange("v u e p -> v u p e"))
-            for u in range(2):
-                turn_back(back[h][:, u], rounded[h][:, u])
-        for h in (1, 0):
-            nc.scalar.copy(words(x_bf0[h][:]), back[h][:].rearrange("p u v -> p v u"))
-
-        for h in (1, 0):
-            ids = slice(h * VH, (h + 1) * VH)
-            nc.vector.tensor_tensor(
-                x_bf1[:, ids],
-                sums[0][:, :, ids].rearrange("p u v e -> p v u e"),
-                sums[1][:, :, ids].rearrange("p u v e -> p v u e"),
-                ADD,
-            )
-        cast_weights(nc.vector.tensor_copy, slice(M // 4, M))
-        x_codes = {1: keep.tile([P, V], U32, name="x_codes1", align_bytes=64)}
-        quantize_x(1, 0, V, x_bf1[:])
-        w_codes = keep.tile([P, PASSES, M], U32, name="w_codes", tag="sums0", align_bytes=64)
+        nc.vector.tensor_copy(
+            w_bf[:].rearrange("p g (c i) t -> p g c t i", i=4),
+            w_raw[:].rearrange("p g t (c i) -> p g c t i", i=4),
+        )
+        quantize_x(0, 0, V, x_bf0[:])
         nc.vector.quantize_mx(
             out=w_codes[:].rearrange("p g m -> p (g m)").bitcast(FP8X4),
             scales=w_scales[:].rearrange("p g m -> p (g m)"),
-            in_=w_bf.rearrange("p g m t -> p (g m t)"),
+            in_=w_bf[:].rearrange("p g m t -> p (g m t)"),
         )
-        x_codes[0] = keep.tile([P, V], U32, name="x_codes0", tag="pair1", align_bytes=64)
-        quantize_x(0, VH, V, x_bf0[1][:])
-        quantize_x(0, 0, VH, x_bf0[0][:])
+
+        rounded = [keep.tile([P, 2, P, 2], BF16, name=f"rounded{h}", align_bytes=64) for h in range(2)]
+        back = [psum.tile([P, 2, VH], F32, name=f"back{h}") for h in range(2)]
+        x_bf1 = [keep.tile([P, VH, 4], BF16, name=f"x_bf1_{h}", align_bytes=64) for h in range(2)]
+        for h in (1, 0):
+            nc.scalar.copy(rounded[h][:], turned[h][:].rearrange("v (u e) p -> v u p e", e=2))
+            for u in range(2):
+                nc.tensor.transpose(back[h][:, u], rounded[h][:, u].rearrange("v p e -> v (p e)").bitcast(F32), ident[:])
+        for h in (1, 0):
+            nc.scalar.copy(
+                x_bf1[h][:].rearrange("p v t -> p (v t)").bitcast(F32).rearrange("p (v u) -> p v u", u=2),
+                back[h][:].rearrange("p u v -> p v u"),
+            )
+        for h in (1, 0):
+            quantize_x(1, h * VH, (h + 1) * VH, x_bf1[h][:])
+
         acc = [psum.tile([M, VH], F32, name=f"acc{h}", tag=("turned_h0", "back1")[h]) for h in range(2)]
-        for h in (1, 0):
-            multiply(1, h, True)
-        for h in (1, 0):
-            multiply(0, h, False)
+        for g in range(PASSES):
+            for h in (1, 0):
+                ids = slice(h * VH, (h + 1) * VH)
+                nc.tensor.matmul_mx(
+                    out=acc[h][:],
+                    lhsT=w_codes[:, g, :].bitcast(FP8X4),
+                    lhsT_scale=w_scales[:, g, :],
+                    rhs=x_codes[g][:, ids].bitcast(FP8X4),
+                    rhs_scale=x_scales[:, g, ids],
+                    start=(g == 0),
+                    stop=(g == PASSES - 1),
+                )
+        result = [keep.tile([M, VH], F32, name=f"result{h}") for h in range(2)]
         nc.scalar.copy(result[1][:], acc[1][:])
         nc.vector.tensor_copy(result[0][:], acc[0][:])
         for h in (1, 0):

@@ -61,9 +61,9 @@ def tile_picked_hash_lin_none_sub_l_kernel(tc, xT, w, offs, out):
             nc.gpsimd.tensor_tensor(part[:, t].rearrange("p a v -> p (a v)"), got[:, : 2 * V], got[:, 2 * V :], ADD)
         x_bf0 = keep.tile([P, V, 4], BF16, name="x_bf0", align_bytes=64)
         nc.gpsimd.tensor_tensor(
-            x_bf0[:].rearrange("p (c i) t -> p c t i", i=4),
-            part[:, :, 0].rearrange("p t (c i) -> p c t i", i=4),
-            part[:, :, 1].rearrange("p t (c i) -> p c t i", i=4),
+            x_bf0[:],
+            part[:, :, 0].rearrange("p t v -> p v t"),
+            part[:, :, 1].rearrange("p t v -> p v t"),
             ADD,
         )
 
@@ -78,27 +78,21 @@ def tile_picked_hash_lin_none_sub_l_kernel(tc, xT, w, offs, out):
             )
             done.append(h)
 
-        for t in range(3):
-            for on_scalar, r0 in ((True, 0), (False, 4)):
-                got = look_up(on_scalar, 1, t, r0, r0 + 4)
-                for r in range(4):
-                    turn(t, r0 + r, got[:, r * VH : (r + 1) * VH])
-        last = {}
-        for h in (1, 0):
-            for a in range(2):
-                for on_scalar, d in ((True, a), (False, 2 + a)):
-                    r = 2 * d + h
-                    last[r] = look_up(on_scalar, 1, 3, r, r + 1)
-                    turn(3, r, last[r][:])
+        for t, runs in ((0, 4), (1, 4), (2, 2)):
+            for first in range(0, 4, runs):
+                for on_scalar, r0 in ((True, first), (False, 4 + first)):
+                    got = look_up(on_scalar, 1, t, r0, r0 + runs)
+                    for r in range(runs):
+                        turn(t, r0 + r, got[:, r * VH : (r + 1) * VH])
+        for h, on_scalar in ((1, (True, True, False, True)), (0, (False, True, False, True))):
+            for d in range(D):
+                r = 2 * d + h
+                turn(3, r, look_up(on_scalar[d], 1, 3, r, r + 1)[:])
 
         x_scales = keep.tile([P, PASSES, V], U8, name="x_scales", align_bytes=64)
         w_scales = keep.tile([P, PASSES, M], U8, name="w_scales", align_bytes=64)
         w_bf = keep.tile([P, PASSES, M, 4], BF16, name="w_bf", align_bytes=64)
-        w_codes = keep.tile([P, PASSES, M], U32, name="w_codes", align_bytes=64)
-        x_codes = [
-            keep.tile([P, V], U32, name="x_codes0", tag="got1_3_1", align_bytes=64),
-            keep.tile([P, V], U32, name="x_codes1", align_bytes=64),
-        ]
+        x_codes = {0: keep.tile([P, V], U32, name="x_codes0", tag="got1_3_6", align_bytes=64)}
 
         def quantize_x(g, v0, v1, src):
             nc.vector.quantize_mx(
@@ -111,20 +105,21 @@ def tile_picked_hash_lin_none_sub_l_kernel(tc, xT, w, offs, out):
             w_bf[:].rearrange("p g (c i) t -> p g c t i", i=4),
             w_raw[:].rearrange("p g t (c i) -> p g c t i", i=4),
         )
+        rounded = [keep.tile([P, 2, P, 2], BF16, name=f"rounded{h}", align_bytes=64) for h in range(2)]
+        back = [psum.tile([P, 2, VH], F32, name=f"back{h}") for h in range(2)]
+        x_bf1 = [keep.tile([P, VH, 4], BF16, name=f"x_bf1_{h}", align_bytes=64) for h in range(2)]
+        for h, copy in ((1, nc.scalar.copy), (0, nc.vector.tensor_copy)):
+            copy(rounded[h][:], turned[h][:].rearrange("v (u e) p -> v u p e", e=2))
+            for u in range(2):
+                nc.tensor.transpose(back[h][:, u], rounded[h][:, u].rearrange("v p e -> v (p e)").bitcast(F32), ident[:])
         quantize_x(0, 0, V, x_bf0[:])
+        w_codes = keep.tile([P, PASSES, M], U32, name="w_codes", tag="got1_3_4", align_bytes=64)
         nc.vector.quantize_mx(
             out=w_codes[:].rearrange("p g m -> p (g m)").bitcast(FP8X4),
             scales=w_scales[:].rearrange("p g m -> p (g m)"),
             in_=w_bf[:].rearrange("p g m t -> p (g m t)"),
         )
-
-        rounded = [keep.tile([P, 2, P, 2], BF16, name=f"rounded{h}", align_bytes=64) for h in range(2)]
-        back = [psum.tile([P, 2, VH], F32, name=f"back{h}") for h in range(2)]
-        x_bf1 = [keep.tile([P, VH, 4], BF16, name=f"x_bf1_{h}", align_bytes=64) for h in range(2)]
-        for h in (1, 0):
-            nc.scalar.copy(rounded[h][:], turned[h][:].rearrange("v (u e) p -> v u p e", e=2))
-            for u in range(2):
-                nc.tensor.transpose(back[h][:, u], rounded[h][:, u].rearrange("v p e -> v (p e)").bitcast(F32), ident[:])
+        x_codes[1] = keep.tile([P, V], U32, name="x_codes1", tag="x_bf0", align_bytes=64)
         for h in (1, 0):
             nc.scalar.copy(
                 x_bf1[h][:].rearrange("p v t -> p (v t)").bitcast(F32).rearrange("p (v u) -> p v u", u=2),
@@ -133,7 +128,7 @@ def tile_picked_hash_lin_none_sub_l_kernel(tc, xT, w, offs, out):
         for h in (1, 0):
             quantize_x(1, h * VH, (h + 1) * VH, x_bf1[h][:])
 
-        acc = [psum.tile([M, VH], F32, name=f"acc{h}", tag=("turned_h0", "back1")[h]) for h in range(2)]
+        acc = [psum.tile([M, VH], F32, name=f"acc{h}", tag=f"back{h}") for h in range(2)]
         for g in range(PASSES):
             for h in (1, 0):
                 ids = slice(h * VH, (h + 1) * VH)

@@ -61,9 +61,9 @@ def tile_picked_hash_lin_none_sub_l_kernel(tc, xT, w, offs, out):
             nc.gpsimd.tensor_tensor(part[:, t].rearrange("p a v -> p (a v)"), got[:, : 2 * V], got[:, 2 * V :], ADD)
         x_bf0 = keep.tile([P, V, 4], BF16, name="x_bf0", align_bytes=64)
         nc.gpsimd.tensor_tensor(
-            x_bf0[:],
-            part[:, :, 0].rearrange("p t v -> p v t"),
-            part[:, :, 1].rearrange("p t v -> p v t"),
+            x_bf0[:].rearrange("p (c i) t -> p c t i", i=4),
+            part[:, :, 0].rearrange("p t (c i) -> p c t i", i=4),
+            part[:, :, 1].rearrange("p t (c i) -> p c t i", i=4),
             ADD,
         )
 

@@ -18,19 +18,21 @@ COPY = mybir.ActivationFunctionType.Copy
 P = 128
 PASSES = 2
 VH = V // 2
-CUT = 480
+CUTS = (480, 480, 448, 448)
+CAST = 40
 
 
 def tile_picked_hash_lin_none_sub_l_kernel(tc, xT, w, offs, out):
     nc = tc.nc
     with ExitStack() as ctx:
         keep = ctx.enter_context(tc.tile_pool(name="keep", bufs=1))
+        reuse = ctx.enter_context(tc.tile_pool(name="reuse", bufs=1))
         psum = ctx.enter_context(tc.psum_pool(name="psum", bufs=1))
 
         offsets = keep.tile([P, D * V // 16], U16, name="offsets")
         rows = xT.rearrange("(g p t) c -> g t p c", g=PASSES, t=4)
         table = {(g, t): keep.tile([P, T], F32, name=f"table{g}_{t}", align_bytes=64) for g in range(PASSES) for t in range(4)}
-        w_raw = keep.tile([P, PASSES, 4, M], F32, name="w_raw")
+        w_raw = reuse.tile([P, PASSES, 4, M], F32, name="w_raw", offset=0, align_bytes=64)
         for g in range(PASSES):
             for t in range(4):
                 nc.sync.dma_start(out=table[g, t][:], in_=rows[g, t])
@@ -45,7 +47,10 @@ def tile_picked_hash_lin_none_sub_l_kernel(tc, xT, w, offs, out):
         make_identity(nc, ident[:], nomemset=True)
 
         def look_up(on_scalar, g, t, r0, r1):
-            got = keep.tile([P, (r1 - r0) * VH], F32, name=f"got{g}_{t}_{r0}", align_bytes=64)
+            if (t, r0) == (3, 1):
+                got = reuse.tile([P, VH], F32, name="got_first", offset=6144, align_bytes=64)
+            else:
+                got = keep.tile([P, (r1 - r0) * VH], F32, name=f"got{g}_{t}_{r0}", align_bytes=64)
             window = table[g, t][:].indirect(offsets[:, r0 * VH // 16 : r1 * VH // 16])
             if on_scalar:
                 nc.scalar.activation(got[:], window, COPY)
@@ -56,8 +61,9 @@ def tile_picked_hash_lin_none_sub_l_kernel(tc, xT, w, offs, out):
         part = keep.tile([P, 4, 2, V], F32, name="part", align_bytes=64)
         for t in range(4):
             got = keep.tile([P, D * V], F32, name=f"got0_{t}", align_bytes=64)
-            nc.scalar.activation(got[:, :CUT], table[0, t][:].indirect(offsets[:, : CUT // 16]), COPY)
-            nc.vector.tensor_copy(got[:, CUT:], table[0, t][:].indirect(offsets[:, CUT // 16 :]))
+            cut = CUTS[t]
+            nc.scalar.activation(got[:, :cut], table[0, t][:].indirect(offsets[:, : cut // 16]), COPY)
+            nc.vector.tensor_copy(got[:, cut:], table[0, t][:].indirect(offsets[:, cut // 16 :]))
             nc.gpsimd.tensor_tensor(part[:, t].rearrange("p a v -> p (a v)"), got[:, : 2 * V], got[:, 2 * V :], ADD)
         x_bf0 = keep.tile([P, V, 4], BF16, name="x_bf0", align_bytes=64)
         nc.gpsimd.tensor_tensor(
@@ -67,16 +73,16 @@ def tile_picked_hash_lin_none_sub_l_kernel(tc, xT, w, offs, out):
             ADD,
         )
 
-        turned = [psum.tile([P, 4, P], F32, name=f"turned_h{h}") for h in range(2)]
+        turned = {(u, h): psum.tile([P, 2, P], F32, name=f"turned{u}_h{h}") for u in range(2) for h in range(2)}
         done = []
 
         def turn(t, r, term):
-            h = r % 2
+            bank = (t // 2, r % 2)
             nc.tensor.matmul(
-                turned[h][:, t, :], term, ident[:],
-                is_transpose=True, start=(done.count(h) == 0), stop=(done.count(h) == 4 * D - 1),
+                turned[bank][:, t % 2, :], term, ident[:],
+                is_transpose=True, start=(done.count(bank) == 0), stop=(done.count(bank) == 2 * D - 1),
             )
-            done.append(h)
+            done.append(bank)
 
         for t, runs in ((0, 4), (1, 4), (2, 2)):
             for first in range(0, 4, runs):
@@ -91,8 +97,8 @@ def tile_picked_hash_lin_none_sub_l_kernel(tc, xT, w, offs, out):
 
         x_scales = keep.tile([P, PASSES, V], U8, name="x_scales", align_bytes=64)
         w_scales = keep.tile([P, PASSES, M], U8, name="w_scales", align_bytes=64)
-        w_bf = keep.tile([P, PASSES, M, 4], BF16, name="w_bf", align_bytes=64)
-        x_codes = {0: keep.tile([P, V], U32, name="x_codes0", tag="got1_3_6", align_bytes=64)}
+        w_bf = keep.tile([P, PASSES, M, 4], BF16, name="w_bf", tag="got1_3_7", align_bytes=64)
+        x_codes = {0: reuse.tile([P, V], U32, name="x_codes0", offset=1024, align_bytes=64)}
 
         def quantize_x(g, v0, v1, src):
             nc.vector.quantize_mx(
@@ -101,19 +107,36 @@ def tile_picked_hash_lin_none_sub_l_kernel(tc, xT, w, offs, out):
                 in_=src.rearrange("p v t -> p (v t)"),
             )
 
-        nc.vector.tensor_copy(
-            w_bf[:].rearrange("p g (c i) t -> p g c t i", i=4),
-            w_raw[:].rearrange("p g t (c i) -> p g c t i", i=4),
-        )
-        rounded = [keep.tile([P, 2, P, 2], BF16, name=f"rounded{h}", align_bytes=64) for h in range(2)]
+        rounded = {
+            (0, 0): reuse.tile([P, P, 2], BF16, name="rounded0_h0", offset=6400, align_bytes=64),
+            (0, 1): reuse.tile([P, P, 2], BF16, name="rounded0_h1", offset=5888, align_bytes=64),
+            (1, 0): keep.tile([P, P, 2], BF16, name="rounded1_h0", align_bytes=64),
+            (1, 1): keep.tile([P, P, 2], BF16, name="rounded1_h1", align_bytes=64),
+        }
         back = [psum.tile([P, 2, VH], F32, name=f"back{h}") for h in range(2)]
         x_bf1 = [keep.tile([P, VH, 4], BF16, name=f"x_bf1_{h}", align_bytes=64) for h in range(2)]
+
+        def round_sums(copy, u, h):
+            copy(rounded[u, h][:], turned[u, h][:].rearrange("v e p -> v p e"))
+
+        def turn_back(u, h):
+            nc.tensor.transpose(back[h][:, u], rounded[u, h][:].rearrange("v p e -> v (p e)").bitcast(F32), ident[:])
+
+        def cast_weights(copy, cols):
+            copy(
+                w_bf[:, :, cols].rearrange("p g (c i) t -> p g c t i", i=4),
+                w_raw[:, :, :, cols].rearrange("p g t (c i) -> p g c t i", i=4),
+            )
+
         for h, copy in ((1, nc.scalar.copy), (0, nc.vector.tensor_copy)):
-            copy(rounded[h][:], turned[h][:].rearrange("v (u e) p -> v u p e", e=2))
             for u in range(2):
-                nc.tensor.transpose(back[h][:, u], rounded[h][:, u].rearrange("v p e -> v (p e)").bitcast(F32), ident[:])
+                round_sums(copy, u, h)
+            for u in (1, 0):
+                turn_back(u, h)
+        cast_weights(nc.scalar.copy, slice(0, CAST))
+        cast_weights(nc.vector.tensor_copy, slice(CAST, M))
         quantize_x(0, 0, V, x_bf0[:])
-        w_codes = keep.tile([P, PASSES, M], U32, name="w_codes", tag="got1_3_4", align_bytes=64)
+        w_codes = keep.tile([P, PASSES, M], U32, name="w_codes", align_bytes=64)
         nc.vector.quantize_mx(
             out=w_codes[:].rearrange("p g m -> p (g m)").bitcast(FP8X4),
             scales=w_scales[:].rearrange("p g m -> p (g m)"),
@@ -129,8 +152,8 @@ def tile_picked_hash_lin_none_sub_l_kernel(tc, xT, w, offs, out):
             quantize_x(1, h * VH, (h + 1) * VH, x_bf1[h][:])
 
         acc = [psum.tile([M, VH], F32, name=f"acc{h}", tag=f"back{h}") for h in range(2)]
-        for g in range(PASSES):
-            for h in (1, 0):
+        for h in (1, 0):
+            for g in range(PASSES):
                 ids = slice(h * VH, (h + 1) * VH)
                 nc.tensor.matmul_mx(
                     out=acc[h][:],

@@ -19,7 +19,7 @@ P = 128
 PASSES = 2
 VH = V // 2
 CUTS = (480, 480, 448, 448)
-CAST = 40
+CAST = 32
 
 
 def tile_picked_hash_lin_none_sub_l_kernel(tc, xT, w, offs, out):
@@ -131,9 +131,9 @@ def tile_picked_hash_lin_none_sub_l_kernel(tc, xT, w, offs, out):
         for h, copy in ((1, nc.scalar.copy), (0, nc.vector.tensor_copy)):
             for u in range(2):
                 round_sums(copy, u, h)
-            for u in (1, 0):
+            for u in range(2):
                 turn_back(u, h)
-        cast_weights(nc.scalar.copy, slice(0, CAST))
+        nc.scalar.copy(w_bf[:, :, :CAST], w_raw[:, :, :, :CAST].rearrange("p g t m -> p g m t"))
         cast_weights(nc.vector.tensor_copy, slice(CAST, M))
         quantize_x(0, 0, V, x_bf0[:])
         w_codes = keep.tile([P, PASSES, M], U32, name="w_codes", align_bytes=64)

@@ -18,7 +18,7 @@ COPY = mybir.ActivationFunctionType.Copy
 P = 128
 PASSES = 2
 VH = V // 2
-CUTS = (480, 480, 448, 448)
+CUT = 480
 CAST = 32
 
 
@@ -61,7 +61,7 @@ def tile_picked_hash_lin_none_sub_l_kernel(tc, xT, w, offs, out):
         part = keep.tile([P, 4, 2, V], F32, name="part", align_bytes=64)
         for t in range(4):
             got = keep.tile([P, D * V], F32, name=f"got0_{t}", align_bytes=64)
-            cut = CUTS[t]
+            cut = CUT
             nc.scalar.activation(got[:, :cut], table[0, t][:].indirect(offsets[:, : cut // 16]), COPY)
             nc.vector.tensor_copy(got[:, cut:], table[0, t][:].indirect(offsets[:, cut // 16 :]))
             nc.gpsimd.tensor_tensor(part[:, t].rearrange("p a v -> p (a v)"), got[:, : 2 * V], got[:, 2 * V :], ADD)
@@ -90,10 +90,20 @@ def tile_picked_hash_lin_none_sub_l_kernel(tc, xT, w, offs, out):
                     got = look_up(on_scalar, 1, t, r0, r0 + runs)
                     for r in range(runs):
                         turn(t, r0 + r, got[:, r * VH : (r + 1) * VH])
-        for h, on_scalar in ((1, (True, True, False, True)), (0, (False, True, False, True))):
-            for d in range(D):
-                r = 2 * d + h
-                turn(3, r, look_up(on_scalar[d], 1, 3, r, r + 1)[:])
+        def entries(first, count):
+            return table[1, 3][:].indirect(offsets[:, first // 16 : (first + count) // 16])
+
+        both = keep.tile([P, 2 * VH], F32, name="got_both", align_bytes=64)
+        for r in (1, 3):
+            turn(3, r, look_up(True, 1, 3, r, r + 1)[:])
+        nc.vector.tensor_copy(both[:, VH // 2 :], entries(4 * VH + VH // 2, VH + VH // 2))
+        turn(3, 5, both[:, VH:])
+        for on_scalar, r in ((True, 7), (False, 0)):
+            turn(3, r, look_up(on_scalar, 1, 3, r, r + 1)[:])
+        nc.scalar.activation(both[:, : VH // 2], entries(4 * VH, VH // 2), COPY)
+        turn(3, 4, both[:, :VH])
+        for on_scalar, r in ((False, 6), (True, 2)):
+            turn(3, r, look_up(on_scalar, 1, 3, r, r + 1)[:])
 
         x_scales = keep.tile([P, PASSES, V], U8, name="x_scales", align_bytes=64)
         w_scales = keep.tile([P, PASSES, M], U8, name="w_scales", align_bytes=64)

from contextlib import ExitStack

import concourse.mybir as mybir
from concourse.masks import make_identity

K, T, D, V, M = 1024, 1024, 4, 256, 128
FLOPS = 2 * K * V * M

F32 = mybir.dt.float32
BF16 = mybir.dt.bfloat16
U32 = mybir.dt.uint32
U16 = mybir.dt.uint16
U8 = mybir.dt.uint8
FP8X4 = mybir.dt.float8_e4m3fn_x4
ADD = mybir.AluOpType.add
COPY = mybir.ActivationFunctionType.Copy

P = 128
PASSES = 2
VH = V // 2
CUT = 480
CAST = 32


def tile_picked_hash_lin_none_sub_l_kernel(tc, xT, w, offs, out):
    nc = tc.nc
    with ExitStack() as ctx:
        keep = ctx.enter_context(tc.tile_pool(name="keep", bufs=1))
        reuse = ctx.enter_context(tc.tile_pool(name="reuse", bufs=1))
        psum = ctx.enter_context(tc.psum_pool(name="psum", bufs=1))

        offsets = keep.tile([P, D * V // 16], U16, name="offsets")
        rows = xT.rearrange("(g p t) c -> g t p c", g=PASSES, t=4)
        table = {(g, t): keep.tile([P, T], F32, name=f"table{g}_{t}", align_bytes=64) for g in range(PASSES) for t in range(4)}
        w_raw = reuse.tile([P, PASSES, 4, M], F32, name="w_raw", offset=0, align_bytes=64)
        for g in range(PASSES):
            for t in range(4):
                nc.sync.dma_start(out=table[g, t][:], in_=rows[g, t])
                if (g, t) == (0, 0):
                    nc.sync.dma_start(offsets[:], offs)
        nc.sync.dma_start(out=w_raw[:], in_=w.rearrange("(g p t) m -> p g t m", g=PASSES, t=4))

        ident = keep.tile([P, P], F32, name="ident")
        zeros = keep.tile([P, P], F32, name="zeros")
        nc.vector.memset(zeros[:], 0.0)
        nc.scalar.copy(ident[:], zeros[:])
        make_identity(nc, ident[:], nomemset=True)

        def look_up(on_scalar, g, t, r0, r1):
            if (t, r0) == (3, 1):
                got = reuse.tile([P, VH], F32, name="got_first", offset=6144, align_bytes=64)
            else:
                got = keep.tile([P, (r1 - r0) * VH], F32, name=f"got{g}_{t}_{r0}", align_bytes=64)
            window = table[g, t][:].indirect(offsets[:, r0 * VH // 16 : r1 * VH // 16])
            if on_scalar:
                nc.scalar.activation(got[:], window, COPY)
            else:
                nc.vector.tensor_copy(got[:], window)
            return got

        part = keep.tile([P, 4, 2, V], F32, name="part", align_bytes=64)
        for t in range(4):
            got = keep.tile([P, D * V], F32, name=f"got0_{t}", align_bytes=64)
            cut = CUT
            nc.scalar.activation(got[:, :cut], table[0, t][:].indirect(offsets[:, : cut // 16]), COPY)
            nc.vector.tensor_copy(got[:, cut:], table[0, t][:].indirect(offsets[:, cut // 16 :]))
            nc.gpsimd.tensor_tensor(part[:, t].rearrange("p a v -> p (a v)"), got[:, : 2 * V], got[:, 2 * V :], ADD)
        x_bf0 = keep.tile([P, V, 4], BF16, name="x_bf0", align_bytes=64)
        nc.gpsimd.tensor_tensor(
            x_bf0[:].rearrange("p (c i) t -> p c t i", i=4),
            part[:, :, 0].rearrange("p t (c i) -> p c t i", i=4),
            part[:, :, 1].rearrange("p t (c i) -> p c t i", i=4),
            ADD,
        )

        turned = {(u, h): psum.tile([P, 2, P], F32, name=f"turned{u}_h{h}") for u in range(2) for h in range(2)}
        done = []

        def turn(t, r, term):
            bank = (t // 2, r % 2)
            nc.tensor.matmul(
                turned[bank][:, t % 2, :], term, ident[:],
                is_transpose=True, start=(done.count(bank) == 0), stop=(done.count(bank) == 2 * D - 1),
            )
            done.append(bank)

        for t, runs in ((0, 4), (1, 4), (2, 2)):
            for first in range(0, 4, runs):
                for on_scalar, r0 in ((True, first), (False, 4 + first)):
                    got = look_up(on_scalar, 1, t, r0, r0 + runs)
                    for r in range(runs):
                        turn(t, r0 + r, got[:, r * VH : (r + 1) * VH])
        def entries(first, count):
            return table[1, 3][:].indirect(offsets[:, first // 16 : (first + count) // 16])

        both = keep.tile([P, 2 * VH], F32, name="got_both", align_bytes=64)
        for r in (1, 3):
            turn(3, r, look_up(True, 1, 3, r, r + 1)[:])
        nc.vector.tensor_copy(both[:, VH // 2 :], entries(4 * VH + VH // 2, VH + VH // 2))
        turn(3, 5, both[:, VH:])
        for on_scalar, r in ((True, 7), (False, 0)):
            turn(3, r, look_up(on_scalar, 1, 3, r, r + 1)[:])
        nc.scalar.activation(both[:, : VH // 2], entries(4 * VH, VH // 2), COPY)
        turn(3, 4, both[:, :VH])
        for on_scalar, r in ((False, 6), (True, 2)):
            turn(3, r, look_up(on_scalar, 1, 3, r, r + 1)[:])

        x_scales = keep.tile([P, PASSES, V], U8, name="x_scales", align_bytes=64)
        w_scales = keep.tile([P, PASSES, M], U8, name="w_scales", align_bytes=64)
        w_bf = keep.tile([P, PASSES, M, 4], BF16, name="w_bf", tag="got1_3_7", align_bytes=64)
        x_codes = {0: reuse.tile([P, V], U32, name="x_codes0", offset=1024, align_bytes=64)}

        def quantize_x(g, v0, v1, src):
            nc.vector.quantize_mx(
                out=x_codes[g][:, v0:v1].bitcast(FP8X4),
                scales=x_scales[:, g, v0:v1],
                in_=src.rearrange("p v t -> p (v t)"),
            )

        rounded = {
            (0, 0): reuse.tile([P, P, 2], BF16, name="rounded0_h0", offset=6400, align_bytes=64),
            (0, 1): reuse.tile([P, P, 2], BF16, name="rounded0_h1", offset=5888, align_bytes=64),
            (1, 0): keep.tile([P, P, 2], BF16, name="rounded1_h0", align_bytes=64),
            (1, 1): keep.tile([P, P, 2], BF16, name="rounded1_h1", align_bytes=64),
        }
        back = [psum.tile([P, 2, VH], F32, name=f"back{h}") for h in range(2)]
        x_bf1 = [keep.tile([P, VH, 4], BF16, name=f"x_bf1_{h}", align_bytes=64) for h in range(2)]

        def round_sums(copy, u, h):
            copy(rounded[u, h][:], turned[u, h][:].rearrange("v e p -> v p e"))

        def turn_back(u, h):
            nc.tensor.transpose(back[h][:, u], rounded[u, h][:].rearrange("v p e -> v (p e)").bitcast(F32), ident[:])

        def cast_weights(copy, cols):
            copy(
                w_bf[:, :, cols].rearrange("p g (c i) t -> p g c t i", i=4),
                w_raw[:, :, :, cols].rearrange("p g t (c i) -> p g c t i", i=4),
            )

        for h, copy in ((1, nc.scalar.copy), (0, nc.vector.tensor_copy)):
            for u in range(2):
                round_sums(copy, u, h)
            for u in range(2):
                turn_back(u, h)
        nc.scalar.copy(w_bf[:, :, :CAST], w_raw[:, :, :, :CAST].rearrange("p g t m -> p g m t"))
        cast_weights(nc.vector.tensor_copy, slice(CAST, M))
        quantize_x(0, 0, V, x_bf0[:])
        w_codes = keep.tile([P, PASSES, M], U32, name="w_codes", align_bytes=64)
        nc.vector.quantize_mx(
            out=w_codes[:].rearrange("p g m -> p (g m)").bitcast(FP8X4),
            scales=w_scales[:].rearrange("p g m -> p (g m)"),
            in_=w_bf[:].rearrange("p g m t -> p (g m t)"),
        )
        x_codes[1] = keep.tile([P, V], U32, name="x_codes1", tag="x_bf0", align_bytes=64)
        for h in (1, 0):
            nc.scalar.copy(
                x_bf1[h][:].rearrange("p v t -> p (v t)").bitcast(F32).rearrange("p (v u) -> p v u", u=2),
                back[h][:].rearrange("p u v -> p v u"),
            )
        for h in (1, 0):
            quantize_x(1, h * VH, (h + 1) * VH, x_bf1[h][:])

        acc = [psum.tile([M, VH], F32, name=f"acc{h}", tag=f"back{h}") for h in range(2)]
        for h in (1, 0):
            for g in range(PASSES):
                ids = slice(h * VH, (h + 1) * VH)
                nc.tensor.matmul_mx(
                    out=acc[h][:],
                    lhsT=w_codes[:, g, :].bitcast(FP8X4),
                    lhsT_scale=w_scales[:, g, :],
                    rhs=x_codes[g][:, ids].bitcast(FP8X4),
                    rhs_scale=x_scales[:, g, ids],
                    start=(g == 0),
                    stop=(g == PASSES - 1),
                )
        result = [keep.tile([M, VH], F32, name=f"result{h}") for h in range(2)]
        nc.scalar.copy(result[1][:], acc[1][:])
        nc.vector.tensor_copy(result[0][:], acc[0][:])
        for h in (1, 0):
            nc.sync.dma_start(out=out[:, h * VH : (h + 1) * VH], in_=result[h][:])
